import numpy as np
import ml_dtypes


def mxq(x, axis, fmt="e4m3"):
    dtype, down = {"e4m3": (ml_dtypes.float8_e4m3fn, 7), "e5m2": (ml_dtypes.float8_e5m2, 14)}[fmt]
    v = np.moveaxis(np.asarray(x, np.float32).astype(ml_dtypes.bfloat16).astype(np.float64), axis, -1)
    blocks = v.reshape(v.shape[:-1] + (-1, 32))
    amax = np.abs(blocks).max(-1, keepdims=True)
    byte = np.maximum(np.where(amax > 0, np.frexp(amax)[1] - 1 + 127, 0) - down, 1)
    scale = np.exp2(byte - 127.0)
    codes = (blocks / scale).astype(np.float32).astype(dtype).astype(np.float64)
    return np.moveaxis((codes * scale).reshape(v.shape), -1, axis)


WIDE = False


def mx_kscale(k):
    if not WIDE:
        return np.ones(k)
    levels = np.array([10, -10, 5, -5, 0])
    if k % 512:
        return np.exp2(np.random.permutation(np.resize(levels, k // 32))).repeat(32)
    a = np.empty((k // 512, 16))
    for p in range(k // 512):
        a[p, :8] = np.random.permutation(np.resize(levels, 8))
        for g in range(8):
            far = levels[np.abs(levels - a[p, g]) >= 10]
            a[p, g + 8] = far[np.random.randint(len(far))]
    return np.exp2(a.ravel()).repeat(32)


BF16 = ml_dtypes.bfloat16


def bf(x):
    return np.asarray(x, np.float32).astype(BF16)


def f64(x):
    return np.asarray(x).astype(np.float64)


E2M1 = np.array([0.0, 0.5, 1.0, 1.5, 2.0, 3.0, 4.0, 6.0, -0.0, -0.5, -1.0, -1.5, -2.0, -3.0, -4.0, -6.0])


def pack_weight(w, fmt):
    k, n = w.shape
    w = f64(bf(w)).reshape(k // 32, 32, n)
    amax = np.abs(w).max(1)
    if fmt == "e4m3":
        byte = np.frexp(amax)[1] - 1 + 127 - 7
    else:
        mant, ex = np.frexp(amax / 6.0)
        byte = np.where(mant > 0.5, ex, ex - 1) + 127
    byte = np.clip(np.where(amax > 0, byte, 1), 1, 254)
    scaled = (w * np.exp2(127.0 - byte)[:, None, :]).reshape(k, n).astype(np.float32)
    by_word = np.ascontiguousarray(scaled.reshape(k // 512, 128, 4, n).transpose(0, 1, 3, 2))
    if fmt == "e4m3":
        words = by_word.astype(ml_dtypes.float8_e4m3fn).view(np.uint8)
    else:
        c = by_word.astype(ml_dtypes.float4_e2m1fn).view(np.uint8) & 0xF
        words = c[..., 0::2] | (c[..., 1::2] << 4)
    return np.ascontiguousarray(words), np.ascontiguousarray(byte.astype(np.uint8).reshape(k // 512, 16, n))


def unpack_weight(words, scales, fmt):
    g, p, n, _ = words.shape
    if fmt == "e4m3":
        vals = np.ascontiguousarray(words).view(ml_dtypes.float8_e4m3fn).astype(np.float64)
    else:
        nib = np.empty((g, p, n, 4), np.uint8)
        nib[..., 0::2] = words & 0xF
        nib[..., 1::2] = words >> 4
        vals = E2M1[nib]
    vals = vals * np.repeat(np.exp2(scales.astype(np.float64) - 127.0), 8, axis=1)[..., None]
    return vals.transpose(0, 1, 3, 2).reshape(g * 512, n)
def pack4(w):
    words, scales = pack_weight(w, "e2m1")
    return words.reshape(words.shape[0], 128, -1), scales


def unpack4(words, scales):
    return unpack_weight(words.reshape(words.shape[0], 128, -1, 2), scales, "e2m1")


H, C, G = 1536, 1024, 512


def setup_inputs():
    s, t = mx_kscale(H), mx_kscale(C)
    x = np.random.standard_normal((H, C)) * s[:, None] * t
    A = np.random.standard_normal((H, H)) / (3 * np.sqrt(H)) / s[:, None] * s
    R = np.random.standard_normal((C, C)) / (3 * np.sqrt(C)) / t[:, None] * t
    B = np.random.standard_normal((H, G)) / np.sqrt(H) / s[:, None]
    transfer_words, transfer_scales = pack4(A)
    reclass_words, reclass_scales = pack4(R)
    bracket_words, bracket_scales = pack4(B)
    return {"x": bf(x),
            "transfer_words": transfer_words, "transfer_scales": transfer_scales,
            "reclass_words": reclass_words, "reclass_scales": reclass_scales,
            "bracket_words": bracket_words, "bracket_scales": bracket_scales,
            "propensity": bf(np.random.uniform(0.5, 1.5, H)),
            "rate": bf(np.random.uniform(0.1, 0.5, (G, C)) / t)}


def reference(x, transfer_words, transfer_scales, reclass_words, reclass_scales, bracket_words, bracket_scales, propensity, rate):
    A = unpack4(transfer_words, transfer_scales)
    R = unpack4(reclass_words, reclass_scales)
    B = unpack4(bracket_words, bracket_scales)
    x0 = f64(x)
    x1 = x0 + (A.T @ mxq(x0, 0, "e4m3"))
    x2 = x1 + f64(propensity)[:, None] * (mxq(x1, 1, "e4m3") @ R)
    return f64(rate) * (B.T @ mxq(x2, 0, "e4m3"))

@@ -1,0 +1,574 @@
+from contextlib import ExitStack
+
+import concourse.mybir as mybir
+from concourse.masks import make_identity
+
+H, C, G = 1536, 1024, 512
+
+F32 = mybir.dt.float32
+BF16 = mybir.dt.bfloat16
+I32 = mybir.dt.int32
+U32 = mybir.dt.uint32
+U8 = mybir.dt.uint8
+FP8X4 = mybir.dt.float8_e4m3fn_x4
+FP4X4 = mybir.dt.float4_e2m1fn_x4
+ADD = mybir.AluOpType.add
+MULT = mybir.AluOpType.mult
+
+FLOPS = 2 * (H * H * C + H * C * C + H * G * C)
+
+P = 128
+PACK = 4
+KP = P * PACK
+HG = H // KP
+CG = C // KP
+N = 512
+
+
+def tile_household_bracket_response_t2_kernel(
+    tc,
+    x,
+    transfer_words,
+    transfer_scales,
+    reclass_words,
+    reclass_scales,
+    bracket_words,
+    bracket_scales,
+    propensity,
+    rate,
+    out,
+):
+    nc = tc.nc
+    with ExitStack() as ctx:
+        keep = ctx.enter_context(tc.tile_pool(name="keep", bufs=1))
+        work = ctx.enter_context(tc.tile_pool(name="work", bufs=3))
+        psum = ctx.enter_context(tc.psum_pool(name="psum", bufs=1))
+        free_banks = list(range(8))
+
+        def kt(shape, dtype, name):
+            return keep.tile(shape, dtype, name=name, align_bytes=64)
+
+        a_sc = kt([P, HG, H], U8, "a_sc")
+        r_sc = kt([P, CG, C], U8, "r_sc")
+        b_sc = kt([P, HG, G], U8, "b_sc")
+        nc.vector.memset(a_sc[:].bitcast(I32), 0)
+        nc.gpsimd.memset(r_sc[:].bitcast(I32), 0)
+        nc.gpsimd.memset(b_sc[:].bitcast(I32), 0)
+        ident = kt([P, P], F32, "ident")
+        make_identity(nc, ident[:])
+
+        def load_scales(tile, dram):
+            view = tile[:].bitcast(I32)
+            for q in range(4):
+                nc.sync.dma_start(
+                    out=view[32 * q : 32 * q + 4, :, :],
+                    in_=dram[:, 4 * q : 4 * q + 4, :].rearrange("k r n -> r k n").bitcast(I32),
+                )
+
+        xt = [[kt([P, PACK, N], BF16, f"x_{g}_{hf}") for hf in range(2)] for g in range(HG)]
+
+        def load_x(g, hf):
+            nc.sync.dma_start(
+                out=xt[g][hf][:],
+                in_=x[KP * g : KP * (g + 1), N * hf : N * (hf + 1)].rearrange("(p t) c -> p t c", t=PACK),
+            )
+
+        a_nat = [kt([P, HG, 2 * KP], U8, f"a_nat_{g}") for g in range(HG)]
+
+        def load_a(g):
+            nc.sync.dma_start(
+                out=a_nat[g][:].bitcast(I32),
+                in_=transfer_words[:, :, 2 * KP * g : 2 * KP * (g + 1)].rearrange("k p n -> p k n").bitcast(I32),
+            )
+
+        load_x(0, 0)
+        load_scales(a_sc, transfer_scales)
+        load_a(0)
+        load_x(1, 0)
+        load_x(2, 0)
+        load_x(0, 1)
+        load_a(1)
+        load_x(1, 1)
+        load_x(2, 1)
+        load_a(2)
+        load_scales(r_sc, reclass_scales)
+        r_w = kt([P, CG, 2 * C], U8, "r_w")
+        nc.sync.dma_start(out=r_w[:].bitcast(I32), in_=reclass_words.rearrange("k p n -> p k n").bitcast(I32))
+        prop = kt([P, HG, PACK], BF16, "prop")
+        nc.sync.dma_start(out=prop[:], in_=propensity.rearrange("(g p t) -> p g t", p=P, t=PACK))
+        load_scales(b_sc, bracket_scales)
+        b_w = kt([P, HG, 2 * G], U8, "b_w")
+        nc.sync.dma_start(out=b_w[:].bitcast(I32), in_=bracket_words.rearrange("k p n -> p k n").bitcast(I32))
+        rate_t = kt([P, 4, C], BF16, "rate_t")
+        nc.sync.dma_start(out=rate_t[:], in_=rate.rearrange("(j p) c -> p j c", p=P))
+
+        a_w = [kt([P, HG, 2 * KP], U8, f"a_w_{g}") for g in range(HG)]
+        a_s = [kt([P, HG, KP], U8, f"a_s_{g}") for g in range(HG)]
+        engines = {"V": nc.vector, "G": nc.gpsimd}
+
+        def k(g, t, e):
+            eng = engines[e]
+            eng.tensor_copy(
+                out=a_w[g][:, :, 2 * P * t : 2 * P * (t + 1)].rearrange("p k (m b) -> p k m b", b=2),
+                in_=a_nat[g][:].rearrange("p k (m t b) -> p k t m b", t=PACK, b=2)[:, :, t, :, :],
+            )
+            eng.tensor_copy(
+                out=a_s[g][:, :, P * t : P * (t + 1)],
+                in_=a_sc[:, :, KP * g : KP * (g + 1)].rearrange("p k (m t) -> p k t m", t=PACK)[:, :, t, :],
+            )
+
+        def interleave(e, out, in_):
+            if e == "V":
+                nc.vector.tensor_copy(out=out, in_=in_)
+            elif e == "S":
+                nc.scalar.copy(out=out, in_=in_)
+            else:
+                nc.gpsimd.tensor_scalar(out=out, in0=in_, scalar1=1.0, scalar2=0.0, op0=MULT, op1=ADD)
+
+        xq = [kt([P, C], U32, f"xq_{g}") for g in range(HG)]
+        xs = [kt([P, C], U8, f"xs_{g}") for g in range(HG)]
+        made = {}
+
+        def get(key, pool, shape, dtype, name, **kw):
+            if key not in made:
+                made[key] = pool.tile(shape, dtype, name=name, **kw)
+            return made[key]
+
+        def a(g, hf, i, e):
+            grouped = get(("xgr", g, hf), work, [P, N, PACK], BF16, "xgr", align_bytes=64, bufs=3)
+            cols = slice(P * i, P * (i + 1))
+            interleave(e, grouped[:, cols, :], xt[g][hf][:, :, cols].rearrange("p t c -> p c t"))
+
+        def b(g, hf, e):
+            nc.vector.quantize_mx(
+                out=xq[g][:, N * hf : N * (hf + 1)].bitcast(FP8X4),
+                scales=xs[g][:, N * hf : N * (hf + 1)],
+                in_=made[("xgr", g, hf)][:].rearrange("p c t -> p (c t)"),
+            )
+
+        banks = {}
+
+        def open_bank(key, shape):
+            n = free_banks.pop(0)
+            tile = psum.tile(shape, F32, name="bank", tag=f"bank{n}")
+            banks[key] = tile, n
+            return tile
+
+        def close_bank(key):
+            tile, n = banks[key]
+            free_banks.append(n)
+            return tile
+
+        x1 = [kt([P, PACK, C], F32, f"x1_{g}") for g in range(HG)]
+
+        def S1(g, hf, t, kk, e):
+            if kk == 0:
+                open_bank((g, hf, t), [P, N])
+            nc.tensor.matmul_mx(
+                out=banks[(g, hf, t)][0][:],
+                lhsT=a_w[g][:, kk, 2 * P * t : 2 * P * (t + 1)].bitcast(FP4X4),
+                lhsT_scale=a_s[g][:, kk, P * t : P * (t + 1)],
+                rhs=xq[kk][:, N * hf : N * (hf + 1)].bitcast(FP8X4),
+                rhs_scale=xs[kk][:, N * hf : N * (hf + 1)],
+                start=(kk == 0),
+                stop=(kk == HG - 1),
+            )
+
+        x1q = [[kt([P, KP], U32, f"x1q_{g}_{hf}") for hf in range(2)] for g in range(HG)]
+        x1s = [[kt([P, KP], U8, f"x1s_{g}_{hf}") for hf in range(2)] for g in range(HG)]
+
+        PERM = "p (w u) -> p u w"
+
+        def c(g, hf, t, e):
+            nc.vector.tensor_tensor(
+                out=x1[g][:, t, N * hf : N * (hf + 1)].rearrange("p (u w) -> p u w", u=PACK),
+                in0=close_bank((g, hf, t))[:].rearrange(PERM, u=PACK),
+                in1=xt[g][hf][:, t, :].rearrange(PERM, u=PACK),
+                op=ADD,
+            )
+
+        def T(g, hf, t, e):
+            bank = open_bank(("T", g, hf, t), [P, PACK, P])
+            for u in range(PACK):
+                nc.tensor.transpose(bank[:, u, :], x1[g][:, t, N * hf + P * u : N * hf + P * (u + 1)], ident[:])
+
+        def e(g, hf, t, e):
+            grouped = get(("x1gr", g, hf), work, [P, KP, PACK], BF16, "x1gr", align_bytes=64, bufs=4)
+            src = close_bank(("T", g, hf, t))[:].rearrange("p u r -> p r u")
+            if e == "S":
+                nc.scalar.copy(out=grouped[:, P * t : P * (t + 1), :], in_=src)
+            else:
+                nc.vector.tensor_copy(out=grouped[:, P * t : P * (t + 1), :], in_=src)
+
+        def f(g, hf, e):
+            nc.vector.quantize_mx(
+                out=x1q[g][hf][:].bitcast(FP8X4),
+                scales=x1s[g][hf][:],
+                in_=made[("x1gr", g, hf)][:].rearrange("p c t -> p (c t)"),
+            )
+
+        def S2(g, hf, t, e):
+            acc = open_bank((2, g, hf, t), [P, N])
+            for kk in range(CG):
+                nc.tensor.matmul_mx(
+                    out=acc[:],
+                    lhsT=x1q[g][kk][:, P * t : P * (t + 1)].bitcast(FP8X4),
+                    lhsT_scale=x1s[g][kk][:, P * t : P * (t + 1)],
+                    rhs=r_w[:, kk, 2 * N * hf : 2 * N * (hf + 1)].bitcast(FP4X4),
+                    rhs_scale=r_sc[:, kk, N * hf : N * (hf + 1)],
+                    start=(kk == 0),
+                    stop=(kk == CG - 1),
+                )
+
+        def g(g, hf, t, e):
+            x2 = get(("x2", g, hf), work, [P, PACK, N], BF16, "x2", align_bytes=64, bufs=3)
+            nc.vector.scalar_tensor_tensor(
+                out=x2[:, t, :].rearrange("p (u w) -> p u w", u=PACK),
+                in0=close_bank((2, g, hf, t))[:].rearrange("p (w u) -> p u w", u=PACK),
+                scalar=prop[:, g, t : t + 1],
+                in1=x1[g][:, t, N * hf : N * (hf + 1)].rearrange("p (u w) -> p u w", u=PACK),
+                op0=MULT,
+                op1=ADD,
+            )
+
+        x2q = [kt([P, C], U32, f"x2q_{g}") for g in range(HG)]
+        x2s = [kt([P, C], U8, f"x2s_{g}") for g in range(HG)]
+
+        def h(g, hf, i, e):
+            grouped = get(("x2gr", g, hf), work, [P, N, PACK], BF16, "x2gr", align_bytes=64, bufs=3)
+            cols = slice(P * i, P * (i + 1))
+            interleave(e, grouped[:, cols, :], made[("x2", g, hf)][:, :, cols].rearrange("p t c -> p c t"))
+
+        def i(g, hf, e):
+            nc.vector.quantize_mx(
+                out=x2q[g][:, N * hf : N * (hf + 1)].bitcast(FP8X4),
+                scales=x2s[g][:, N * hf : N * (hf + 1)],
+                in_=made[("x2gr", g, hf)][:].rearrange("p c t -> p (c t)"),
+            )
+
+        def S3(hf, j, kk, e):
+            if kk == 0:
+                open_bank((3, hf, j), [P, N])
+            nc.tensor.matmul_mx(
+                out=banks[(3, hf, j)][0][:],
+                lhsT=b_w[:, kk, 2 * P * j : 2 * P * (j + 1)].bitcast(FP4X4),
+                lhsT_scale=b_sc[:, kk, P * j : P * (j + 1)],
+                rhs=x2q[kk][:, N * hf : N * (hf + 1)].bitcast(FP8X4),
+                rhs_scale=x2s[kk][:, N * hf : N * (hf + 1)],
+                start=(kk == 0),
+                stop=(kk == HG - 1),
+            )
+
+        def j(hf, j, e):
+            o = work.tile([P, N], F32, name="o", bufs=8)
+            nc.vector.tensor_tensor(
+                out=o[:].rearrange("p (w u) -> p w u", u=PACK),
+                in0=close_bank((3, hf, j))[:].rearrange("p (u w) -> p w u", u=PACK),
+                in1=rate_t[:, j, N * hf : N * (hf + 1)].rearrange("p (w u) -> p w u", u=PACK),
+                op=MULT,
+            )
+            nc.sync.dma_start(out=out[P * j : P * (j + 1), N * hf : N * (hf + 1)], in_=o[:])
+
+        ctx.enter_context(tc.manual_schedule())
+        a(1, 0, 2, "S")
+        a(0, 0, 1, "V")
+        a(0, 0, 0, "V")
+        a(0, 0, 3, "V")
+        a(0, 0, 2, "V")
+        a(1, 0, 0, "S")
+        b(0, 0, "V")
+        k(0, 3, "G")
+        k(0, 2, "V")
+        S1(0, 0, 3, 0, "PE")
+        k(0, 0, "V")
+        S1(0, 0, 2, 0, "PE")
+        k(0, 1, "V")
+        a(1, 0, 1, "V")
+        a(1, 0, 3, "V")
+        S1(0, 0, 1, 0, "PE")
+        k(1, 2, "G")
+        b(1, 0, "V")
+        a(2, 0, 3, "V")
+        S1(0, 0, 0, 0, "PE")
+        S1(0, 0, 0, 1, "PE")
+        a(2, 0, 2, "S")
+        S1(0, 0, 2, 1, "PE")
+        a(2, 0, 0, "S")
+        S1(0, 0, 1, 1, "PE")
+        a(2, 0, 1, "S")
+        S1(0, 0, 3, 1, "PE")
+        k(1, 3, "V")
+        b(2, 0, "V")
+        S1(1, 0, 3, 0, "PE")
+        S1(1, 0, 3, 1, "PE")
+        S1(0, 0, 0, 2, "PE")
+        a(0, 1, 3, "S")
+        a(0, 1, 1, "S")
+        k(1, 1, "V")
+        S1(0, 0, 3, 2, "PE")
+        a(0, 1, 2, "V")
+        S1(1, 0, 1, 0, "PE")
+        S1(1, 0, 1, 1, "PE")
+        S1(1, 0, 2, 0, "PE")
+        c(0, 0, 3, "V")
+        S1(0, 0, 1, 2, "PE")
+        a(1, 1, 0, "S")
+        S1(1, 0, 3, 2, "PE")
+        S1(1, 0, 1, 2, "PE")
+        a(2, 1, 1, "V")
+        a(1, 1, 3, "S")
+        c(0, 0, 1, "V")
+        S1(1, 0, 2, 1, "PE")
+        k(2, 2, "V")
+        S1(0, 0, 2, 2, "PE")
+        T(0, 0, 1, "PE")
+        k(1, 0, "G")
+        c(0, 0, 2, "V")
+        k(2, 0, "G")
+        a(2, 1, 0, "S")
+        a(1, 1, 2, "S")
+        S1(2, 0, 2, 0, "PE")
+        S1(1, 0, 0, 0, "PE")
+        c(1, 0, 1, "V")
+        S1(1, 0, 0, 1, "PE")
+        S1(2, 0, 2, 1, "PE")
+        S1(1, 0, 0, 2, "PE")
+        a(2, 1, 2, "S")
+        S1(2, 0, 0, 0, "PE")
+        k(2, 3, "G")
+        a(0, 1, 0, "S")
+        S1(2, 0, 0, 1, "PE")
+        b(0, 1, "V")
+        a(2, 1, 3, "S")
+        S1(0, 1, 2, 0, "PE")
+        c(0, 0, 0, "V")
+        a(1, 1, 1, "S")
+        S1(2, 0, 2, 2, "PE")
+        b(1, 1, "V")
+        e(0, 0, 1, "S")
+        S1(1, 0, 2, 2, "PE")
+        S1(2, 0, 0, 2, "PE")
+        c(1, 0, 0, "V")
+        S1(1, 1, 2, 0, "PE")
+        S1(0, 1, 0, 0, "PE")
+        S1(1, 1, 2, 1, "PE")
+        c(1, 0, 2, "V")
+        c(1, 0, 3, "V")
+        S1(0, 1, 3, 0, "PE")
+        S1(0, 1, 3, 1, "PE")
+        S1(2, 0, 3, 0, "PE")
+        b(2, 1, "V")
+        S1(0, 1, 1, 0, "PE")
+        c(2, 0, 2, "V")
+        c(2, 0, 0, "V")
+        S1(0, 1, 2, 1, "PE")
+        S1(2, 0, 3, 1, "PE")
+        S1(0, 1, 3, 2, "PE")
+        c(0, 1, 3, "V")
+        k(2, 1, "G")
+        S1(0, 1, 2, 2, "PE")
+        S1(2, 0, 3, 2, "PE")
+        S1(0, 1, 0, 1, "PE")
+        S1(2, 0, 1, 0, "PE")
+        S1(1, 1, 3, 0, "PE")
+        S1(0, 1, 1, 1, "PE")
+        S1(0, 1, 1, 2, "PE")
+        c(0, 1, 1, "V")
+        c(0, 1, 2, "V")
+        S1(1, 1, 2, 2, "PE")
+        S1(2, 1, 1, 0, "PE")
+        S1(2, 1, 1, 1, "PE")
+        S1(1, 1, 3, 1, "PE")
+        S1(2, 0, 1, 1, "PE")
+        S1(0, 1, 0, 2, "PE")
+        c(2, 0, 3, "V")
+        S1(2, 1, 2, 0, "PE")
+        S1(2, 0, 1, 2, "PE")
+        c(2, 0, 1, "V")
+        S1(1, 1, 0, 0, "PE")
+        S1(2, 1, 2, 1, "PE")
+        S1(1, 1, 0, 1, "PE")
+        S1(1, 1, 0, 2, "PE")
+        S1(1, 1, 3, 2, "PE")
+        c(0, 1, 0, "V")
+        S1(2, 1, 2, 2, "PE")
+        c(1, 1, 0, "V")
+        S1(2, 1, 1, 2, "PE")
+        c(2, 1, 2, "V")
+        T(0, 0, 3, "PE")
+        c(1, 1, 3, "V")
+        T(0, 1, 1, "PE")
+        T(0, 1, 0, "PE")
+        c(1, 1, 2, "V")
+        T(0, 1, 3, "PE")
+        e(0, 1, 1, "V")
+        e(0, 1, 0, "S")
+        T(0, 0, 2, "PE")
+        T(2, 0, 1, "PE")
+        T(2, 0, 0, "PE")
+        e(0, 0, 2, "S")
+        T(0, 1, 2, "PE")
+        c(2, 1, 1, "V")
+        e(2, 0, 0, "S")
+        e(0, 1, 3, "S")
+        T(1, 1, 3, "PE")
+        S1(1, 1, 1, 0, "PE")
+        S1(1, 1, 1, 1, "PE")
+        e(0, 0, 3, "S")
+        S1(2, 1, 0, 0, "PE")
+        S1(1, 1, 1, 2, "PE")
+        S1(2, 1, 3, 0, "PE")
+        S1(2, 1, 3, 1, "PE")
+        e(0, 1, 2, "S")
+        S1(2, 1, 0, 1, "PE")
+        S1(2, 1, 3, 2, "PE")
+        c(1, 1, 1, "V")
+        S1(2, 1, 0, 2, "PE")
+        T(2, 0, 3, "PE")
+        T(0, 0, 0, "PE")
+        e(2, 0, 1, "S")
+        f(0, 1, "V")
+        c(2, 1, 0, "V")
+        T(2, 1, 1, "PE")
+        T(2, 1, 2, "PE")
+        T(2, 0, 2, "PE")
+        e(0, 0, 0, "S")
+        T(1, 1, 0, "PE")
+        T(1, 0, 3, "PE")
+        c(2, 1, 3, "V")
+        e(2, 0, 3, "V")
+        e(2, 0, 2, "S")
+        f(0, 0, "V")
+        T(2, 1, 0, "PE")
+        e(2, 1, 0, "S")
+        T(2, 1, 3, "PE")
+        e(1, 1, 0, "V")
+        S2(0, 0, 3, "PE")
+        e(2, 1, 1, "V")
+        e(2, 1, 2, "S")
+        f(2, 0, "V")
+        g(0, 0, 3, "V")
+        S2(0, 1, 2, "PE")
+        g(0, 1, 2, "V")
+        S2(0, 0, 0, "PE")
+        g(0, 0, 0, "V")
+        S2(0, 0, 2, "PE")
+        g(0, 0, 2, "V")
+        e(1, 1, 3, "S")
+        S2(0, 1, 3, "PE")
+        S2(0, 0, 1, "PE")
+        e(1, 0, 3, "S")
+        e(2, 1, 3, "S")
+        T(1, 1, 2, "PE")
+        T(1, 1, 1, "PE")
+        T(1, 0, 1, "PE")
+        T(1, 0, 0, "PE")
+        T(1, 0, 2, "PE")
+        e(1, 1, 2, "S")
+        S2(0, 1, 0, "PE")
+        g(0, 1, 3, "V")
+        f(2, 1, "V")
+        g(0, 0, 1, "V")
+        h(0, 0, 2, "V")
+        S2(0, 1, 1, "PE")
+        e(1, 1, 1, "S")
+        f(1, 1, "V")
+        S2(2, 0, 0, "PE")
+        e(1, 0, 1, "S")
+        h(0, 0, 0, "S")
+        e(1, 0, 2, "S")
+        g(0, 1, 0, "V")
+        g(0, 1, 1, "V")
+        e(1, 0, 0, "S")
+        g(2, 0, 0, "V")
+        h(0, 0, 3, "S")
+        f(1, 0, "V")
+        S2(2, 0, 1, "PE")
+        S2(2, 0, 2, "PE")
+        S2(2, 0, 3, "PE")
+        h(0, 0, 1, "S")
+        S2(1, 0, 3, "PE")
+        g(2, 0, 1, "V")
+        g(2, 0, 2, "V")
+        g(1, 0, 3, "V")
+        S2(1, 0, 2, "PE")
+        S2(1, 0, 1, "PE")
+        g(2, 0, 3, "V")
+        h(0, 1, 3, "S")
+        S2(2, 1, 2, "PE")
+        h(0, 1, 1, "S")
+        i(0, 0, "V")
+        h(0, 1, 0, "S")
+        h(0, 1, 2, "S")
+        S2(1, 0, 0, "PE")
+        g(1, 0, 2, "V")
+        S2(2, 1, 3, "PE")
+        g(1, 0, 0, "V")
+        g(1, 0, 1, "V")
+        g(2, 1, 2, "V")
+        S2(1, 1, 2, "PE")
+        i(0, 1, "V")
+        h(2, 0, 1, "S")
+        g(2, 1, 3, "V")
+        S2(1, 1, 1, "PE")
+        S2(2, 1, 1, "PE")
+        h(2, 0, 3, "S")
+        S2(2, 1, 0, "PE")
+        S2(1, 1, 3, "PE")
+        h(2, 0, 2, "S")
+        S3(1, 0, 0, "PE")
+        S2(1, 1, 0, "PE")
+        S3(0, 0, 0, "PE")
+        h(2, 0, 0, "S")
+        g(2, 1, 0, "V")
+        g(1, 1, 1, "V")
+        S3(0, 2, 0, "PE")
+        S3(1, 3, 0, "PE")
+        h(1, 0, 0, "S")
+        g(1, 1, 3, "V")
+        h(1, 0, 1, "S")
+        h(1, 0, 2, "S")
+        S3(0, 3, 0, "PE")
+        h(1, 0, 3, "S")
+        g(2, 1, 1, "V")
+        h(2, 1, 0, "S")
+        i(1, 0, "V")
+        g(1, 1, 0, "V")
+        S3(0, 0, 1, "PE")
+        S3(0, 1, 0, "PE")
+        S3(1, 1, 0, "PE")
+        g(1, 1, 2, "V")
+        i(2, 0, "V")
+        S3(0, 2, 1, "PE")
+        S3(0, 1, 1, "PE")
+        S3(0, 1, 2, "PE")
+        S3(0, 3, 1, "PE")
+        h(2, 1, 1, "S")
+        h(1, 1, 3, "V")
+        h(2, 1, 3, "S")
+        h(1, 1, 0, "V")
+        S3(1, 2, 0, "PE")
+        h(1, 1, 1, "S")
+        S3(0, 0, 2, "PE")
+        S3(0, 3, 2, "PE")
+        h(1, 1, 2, "S")
+        j(0, 1, "V")
+        i(1, 1, "V")
+        j(0, 0, "V")
+        h(2, 1, 2, "S")
+        i(2, 1, "V")
+        S3(0, 2, 2, "PE")
+        S3(1, 2, 1, "PE")
+        S3(1, 3, 1, "PE")
+        j(0, 2, "V")
+        S3(1, 1, 1, "PE")
+        j(0, 3, "V")
+        S3(1, 0, 1, "PE")
+        S3(1, 2, 2, "PE")
+        S3(1, 1, 2, "PE")
+        S3(1, 3, 2, "PE")
+        j(1, 2, "V")
+        j(1, 1, "V")
+        S3(1, 0, 2, "PE")
+        j(1, 3, "V")
+        j(1, 0, "V")

@@ -177,28 +177,40 @@ def tile_household_bracket_response_t2_kernel(
         x1q = [[kt([P, KP], U32, f"x1q_{g}_{hf}") for hf in range(2)] for g in range(HG)]
         x1s = [[kt([P, KP], U8, f"x1s_{g}_{hf}") for hf in range(2)] for g in range(HG)]
 
-        PERM = "p (w u) -> p u w"
-
         def c(g, hf, t, e):
             nc.vector.tensor_tensor(
-                out=x1[g][:, t, N * hf : N * (hf + 1)].rearrange("p (u w) -> p u w", u=PACK),
-                in0=close_bank((g, hf, t))[:].rearrange(PERM, u=PACK),
-                in1=xt[g][hf][:, t, :].rearrange(PERM, u=PACK),
+                out=x1[g][:, t, N * hf : N * (hf + 1)],
+                in0=close_bank((g, hf, t))[:],
+                in1=xt[g][hf][:, t, :],
                 op=ADD,
             )
 
-        def T(g, hf, t, e):
-            bank = open_bank(("T", g, hf, t), [P, PACK, P])
-            for u in range(PACK):
-                nc.tensor.transpose(bank[:, u, :], x1[g][:, t, N * hf + P * u : N * hf + P * (u + 1)], ident[:])
-
-        def e(g, hf, t, e):
-            grouped = get(("x1gr", g, hf), work, [P, KP, PACK], BF16, "x1gr", align_bytes=64, bufs=4)
-            src = close_bank(("T", g, hf, t))[:].rearrange("p u r -> p r u")
+        def d(g, hf, t, e):
+            xb = get(("xb", g, hf), work, [P, PACK, 2, P, 2], BF16, "xb", align_bytes=64, bufs=4)
+            dst = xb[:, t, :, :, :]
+            src = x1[g][:, t, N * hf : N * (hf + 1)].rearrange("p (w u h) -> p u w h", u=2, h=2)
             if e == "S":
-                nc.scalar.copy(out=grouped[:, P * t : P * (t + 1), :], in_=src)
+                nc.scalar.copy(out=dst, in_=src)
             else:
-                nc.vector.tensor_copy(out=grouped[:, P * t : P * (t + 1), :], in_=src)
+                nc.vector.tensor_copy(out=dst, in_=src)
+
+        def T(g, hf, q, e):
+            bank = open_bank(("T", g, hf, q), [P, 2, 2, P])
+            xb = made[("xb", g, hf)]
+            for t in range(2):
+                for u in range(2):
+                    words = xb[:, 2 * q + t, u, :, :].rearrange("p w h -> p (w h)").bitcast(F32)
+                    nc.tensor.transpose(bank[:, t, u, :], words, ident[:])
+
+        def e(g, hf, q, e):
+            grouped = get(("x1gr", g, hf), work, [P, KP, PACK], BF16, "x1gr", align_bytes=64, bufs=3)
+            dst = grouped[:, 2 * P * q : 2 * P * (q + 1), :].rearrange("p r v -> p (r v)").bitcast(F32)
+            dst = dst.rearrange("p (t r u) -> p t r u", t=2, u=2)
+            src = close_bank(("T", g, hf, q))[:].rearrange("p t u r -> p t r u")
+            if e == "S":
+                nc.scalar.copy(out=dst, in_=src)
+            else:
+                nc.vector.tensor_copy(out=dst, in_=src)
 
         def f(g, hf, e):
             nc.vector.quantize_mx(
@@ -223,10 +235,10 @@ def tile_household_bracket_response_t2_kernel(
         def g(g, hf, t, e):
             x2 = get(("x2", g, hf), work, [P, PACK, N], BF16, "x2", align_bytes=64, bufs=3)
             nc.vector.scalar_tensor_tensor(
-                out=x2[:, t, :].rearrange("p (u w) -> p u w", u=PACK),
-                in0=close_bank((2, g, hf, t))[:].rearrange("p (w u) -> p u w", u=PACK),
+                out=x2[:, t, :],
+                in0=close_bank((2, g, hf, t))[:],
                 scalar=prop[:, g, t : t + 1],
-                in1=x1[g][:, t, N * hf : N * (hf + 1)].rearrange("p (u w) -> p u w", u=PACK),
+                in1=x1[g][:, t, N * hf : N * (hf + 1)],
                 op0=MULT,
                 op1=ADD,
             )
@@ -235,7 +247,7 @@ def tile_household_bracket_response_t2_kernel(
         x2s = [kt([P, C], U8, f"x2s_{g}") for g in range(HG)]
 
         def h(g, hf, i, e):
-            grouped = get(("x2gr", g, hf), work, [P, N, PACK], BF16, "x2gr", align_bytes=64, bufs=3)
+            grouped = get(("x2gr", g, hf), work, [P, N, PACK], BF16, "x2gr", align_bytes=64, bufs=2)
             cols = slice(P * i, P * (i + 1))
             interleave(e, grouped[:, cols, :], made[("x2", g, hf)][:, :, cols].rearrange("p t c -> p c t"))
 
@@ -260,315 +272,315 @@ def tile_household_bracket_response_t2_kernel(
             )
 
         def j(hf, j, e):
-            o = work.tile([P, N], F32, name="o", bufs=8)
+            o = work.tile([P, N], F32, name="o", bufs=7)
             nc.vector.tensor_tensor(
-                out=o[:].rearrange("p (w u) -> p w u", u=PACK),
-                in0=close_bank((3, hf, j))[:].rearrange("p (u w) -> p w u", u=PACK),
-                in1=rate_t[:, j, N * hf : N * (hf + 1)].rearrange("p (w u) -> p w u", u=PACK),
+                out=o[:],
+                in0=close_bank((3, hf, j))[:],
+                in1=rate_t[:, j, N * hf : N * (hf + 1)],
                 op=MULT,
             )
             nc.sync.dma_start(out=out[P * j : P * (j + 1), N * hf : N * (hf + 1)], in_=o[:])
 
         ctx.enter_context(tc.manual_schedule())
         a(1, 0, 2, "S")
-        a(0, 0, 1, "V")
-        a(0, 0, 0, "V")
-        a(0, 0, 3, "V")
-        a(0, 0, 2, "V")
         a(1, 0, 0, "S")
+        a(0, 0, 0, "V")
+        a(1, 0, 3, "S")
+        a(0, 0, 3, "V")
+        a(0, 0, 1, "V")
+        a(0, 0, 2, "V")
         b(0, 0, "V")
-        k(0, 3, "G")
-        k(0, 2, "V")
-        S1(0, 0, 3, 0, "PE")
-        k(0, 0, "V")
-        S1(0, 0, 2, 0, "PE")
         k(0, 1, "V")
-        a(1, 0, 1, "V")
-        a(1, 0, 3, "V")
         S1(0, 0, 1, 0, "PE")
-        k(1, 2, "G")
-        b(1, 0, "V")
-        a(2, 0, 3, "V")
+        k(0, 3, "V")
+        k(0, 2, "V")
+        S1(0, 0, 2, 0, "PE")
+        a(1, 0, 1, "V")
+        k(0, 0, "V")
+        a(2, 0, 3, "S")
         S1(0, 0, 0, 0, "PE")
-        S1(0, 0, 0, 1, "PE")
-        a(2, 0, 2, "S")
-        S1(0, 0, 2, 1, "PE")
+        b(1, 0, "V")
+        S1(0, 0, 3, 0, "PE")
+        k(1, 0, "V")
+        S1(1, 0, 0, 0, "PE")
         a(2, 0, 0, "S")
+        S1(0, 0, 2, 1, "PE")
+        S1(0, 0, 0, 1, "PE")
+        k(1, 2, "V")
         S1(0, 0, 1, 1, "PE")
+        k(1, 1, "V")
+        a(2, 0, 2, "S")
+        S1(1, 0, 2, 0, "PE")
         a(2, 0, 1, "S")
-        S1(0, 0, 3, 1, "PE")
+        a(1, 1, 1, "S")
+        a(1, 1, 0, "S")
+        S1(1, 0, 2, 1, "PE")
         k(1, 3, "V")
+        a(0, 1, 3, "S")
         b(2, 0, "V")
         S1(1, 0, 3, 0, "PE")
-        S1(1, 0, 3, 1, "PE")
-        S1(0, 0, 0, 2, "PE")
-        a(0, 1, 3, "S")
-        a(0, 1, 1, "S")
-        k(1, 1, "V")
-        S1(0, 0, 3, 2, "PE")
-        a(0, 1, 2, "V")
-        S1(1, 0, 1, 0, "PE")
-        S1(1, 0, 1, 1, "PE")
-        S1(1, 0, 2, 0, "PE")
-        c(0, 0, 3, "V")
-        S1(0, 0, 1, 2, "PE")
-        a(1, 1, 0, "S")
-        S1(1, 0, 3, 2, "PE")
-        S1(1, 0, 1, 2, "PE")
-        a(2, 1, 1, "V")
-        a(1, 1, 3, "S")
-        c(0, 0, 1, "V")
-        S1(1, 0, 2, 1, "PE")
-        k(2, 2, "V")
-        S1(0, 0, 2, 2, "PE")
-        T(0, 0, 1, "PE")
-        k(1, 0, "G")
-        c(0, 0, 2, "V")
-        k(2, 0, "G")
-        a(2, 1, 0, "S")
-        a(1, 1, 2, "S")
-        S1(2, 0, 2, 0, "PE")
-        S1(1, 0, 0, 0, "PE")
-        c(1, 0, 1, "V")
         S1(1, 0, 0, 1, "PE")
-        S1(2, 0, 2, 1, "PE")
-        S1(1, 0, 0, 2, "PE")
-        a(2, 1, 2, "S")
-        S1(2, 0, 0, 0, "PE")
-        k(2, 3, "G")
-        a(0, 1, 0, "S")
-        S1(2, 0, 0, 1, "PE")
-        b(0, 1, "V")
-        a(2, 1, 3, "S")
-        S1(0, 1, 2, 0, "PE")
+        S1(0, 0, 3, 1, "PE")
+        S1(0, 0, 3, 2, "PE")
+        S1(0, 0, 0, 2, "PE")
+        k(2, 1, "V")
+        k(2, 3, "V")
+        a(0, 1, 1, "S")
         c(0, 0, 0, "V")
-        a(1, 1, 1, "S")
-        S1(2, 0, 2, 2, "PE")
-        b(1, 1, "V")
-        e(0, 0, 1, "S")
+        S1(2, 0, 1, 0, "PE")
+        S1(2, 0, 1, 1, "PE")
+        a(0, 1, 0, "S")
+        S1(0, 0, 2, 2, "PE")
+        a(2, 1, 1, "S")
+        S1(1, 0, 3, 1, "PE")
+        k(2, 0, "V")
+        S1(2, 0, 1, 2, "PE")
+        c(0, 0, 2, "V")
+        c(2, 0, 1, "V")
+        a(1, 1, 2, "S")
+        a(0, 1, 2, "S")
+        S1(1, 0, 3, 2, "PE")
+        a(2, 1, 2, "S")
+        S1(0, 0, 1, 2, "PE")
+        a(1, 1, 3, "S")
+        k(2, 2, "V")
+        S1(1, 0, 1, 0, "PE")
+        d(0, 0, 2, "S")
+        S1(1, 0, 1, 1, "PE")
+        c(1, 0, 3, "V")
+        b(0, 1, "V")
+        S1(2, 0, 0, 0, "PE")
+        d(0, 0, 0, "S")
+        S1(1, 0, 1, 2, "PE")
+        c(1, 0, 1, "V")
+        a(2, 1, 3, "S")
+        S1(2, 0, 3, 0, "PE")
+        d(1, 0, 1, "S")
+        S1(2, 0, 3, 1, "PE")
         S1(1, 0, 2, 2, "PE")
+        S1(2, 0, 2, 0, "PE")
+        a(2, 1, 0, "S")
+        S1(2, 0, 3, 2, "PE")
+        b(1, 1, "V")
+        c(1, 0, 2, "V")
+        S1(2, 0, 2, 1, "PE")
+        S1(2, 0, 0, 1, "PE")
+        S1(2, 0, 2, 2, "PE")
+        S1(1, 0, 0, 2, "PE")
+        d(1, 0, 2, "S")
         S1(2, 0, 0, 2, "PE")
         c(1, 0, 0, "V")
-        S1(1, 1, 2, 0, "PE")
         S1(0, 1, 0, 0, "PE")
-        S1(1, 1, 2, 1, "PE")
-        c(1, 0, 2, "V")
-        c(1, 0, 3, "V")
+        c(2, 0, 0, "V")
+        S1(0, 1, 0, 1, "PE")
         S1(0, 1, 3, 0, "PE")
         S1(0, 1, 3, 1, "PE")
-        S1(2, 0, 3, 0, "PE")
+        S1(2, 1, 3, 0, "PE")
+        S1(0, 1, 2, 0, "PE")
         b(2, 1, "V")
-        S1(0, 1, 1, 0, "PE")
-        c(2, 0, 2, "V")
-        c(2, 0, 0, "V")
         S1(0, 1, 2, 1, "PE")
-        S1(2, 0, 3, 1, "PE")
+        d(2, 0, 1, "S")
+        c(0, 0, 1, "V")
+        S1(2, 1, 3, 1, "PE")
         S1(0, 1, 3, 2, "PE")
-        c(0, 1, 3, "V")
-        k(2, 1, "G")
-        S1(0, 1, 2, 2, "PE")
-        S1(2, 0, 3, 2, "PE")
-        S1(0, 1, 0, 1, "PE")
-        S1(2, 0, 1, 0, "PE")
-        S1(1, 1, 3, 0, "PE")
-        S1(0, 1, 1, 1, "PE")
-        S1(0, 1, 1, 2, "PE")
-        c(0, 1, 1, "V")
-        c(0, 1, 2, "V")
-        S1(1, 1, 2, 2, "PE")
-        S1(2, 1, 1, 0, "PE")
-        S1(2, 1, 1, 1, "PE")
-        S1(1, 1, 3, 1, "PE")
-        S1(2, 0, 1, 1, "PE")
         S1(0, 1, 0, 2, "PE")
+        c(0, 0, 3, "V")
+        d(2, 0, 0, "S")
         c(2, 0, 3, "V")
-        S1(2, 1, 2, 0, "PE")
-        S1(2, 0, 1, 2, "PE")
-        c(2, 0, 1, "V")
-        S1(1, 1, 0, 0, "PE")
-        S1(2, 1, 2, 1, "PE")
-        S1(1, 1, 0, 1, "PE")
-        S1(1, 1, 0, 2, "PE")
-        S1(1, 1, 3, 2, "PE")
+        d(0, 0, 1, "S")
         c(0, 1, 0, "V")
-        S1(2, 1, 2, 2, "PE")
-        c(1, 1, 0, "V")
-        S1(2, 1, 1, 2, "PE")
-        c(2, 1, 2, "V")
-        T(0, 0, 3, "PE")
-        c(1, 1, 3, "V")
-        T(0, 1, 1, "PE")
-        T(0, 1, 0, "PE")
-        c(1, 1, 2, "V")
-        T(0, 1, 3, "PE")
-        e(0, 1, 1, "V")
-        e(0, 1, 0, "S")
-        T(0, 0, 2, "PE")
-        T(2, 0, 1, "PE")
-        T(2, 0, 0, "PE")
-        e(0, 0, 2, "S")
-        T(0, 1, 2, "PE")
-        c(2, 1, 1, "V")
-        e(2, 0, 0, "S")
-        e(0, 1, 3, "S")
-        T(1, 1, 3, "PE")
         S1(1, 1, 1, 0, "PE")
         S1(1, 1, 1, 1, "PE")
-        e(0, 0, 3, "S")
+        d(0, 0, 3, "S")
+        c(0, 1, 3, "V")
+        S1(0, 1, 1, 0, "PE")
+        S1(1, 1, 2, 0, "PE")
+        S1(0, 1, 1, 1, "PE")
+        S1(0, 1, 1, 2, "PE")
+        S1(0, 1, 2, 2, "PE")
+        c(0, 1, 1, "V")
+        S1(1, 1, 2, 1, "PE")
         S1(2, 1, 0, 0, "PE")
-        S1(1, 1, 1, 2, "PE")
-        S1(2, 1, 3, 0, "PE")
-        S1(2, 1, 3, 1, "PE")
-        e(0, 1, 2, "S")
-        S1(2, 1, 0, 1, "PE")
+        d(1, 0, 0, "S")
+        S1(1, 1, 2, 2, "PE")
         S1(2, 1, 3, 2, "PE")
-        c(1, 1, 1, "V")
-        S1(2, 1, 0, 2, "PE")
-        T(2, 0, 3, "PE")
-        T(0, 0, 0, "PE")
-        e(2, 0, 1, "S")
-        f(0, 1, "V")
-        c(2, 1, 0, "V")
-        T(2, 1, 1, "PE")
-        T(2, 1, 2, "PE")
-        T(2, 0, 2, "PE")
-        e(0, 0, 0, "S")
-        T(1, 1, 0, "PE")
-        T(1, 0, 3, "PE")
-        c(2, 1, 3, "V")
-        e(2, 0, 3, "V")
-        e(2, 0, 2, "S")
-        f(0, 0, "V")
-        T(2, 1, 0, "PE")
-        e(2, 1, 0, "S")
-        T(2, 1, 3, "PE")
-        e(1, 1, 0, "V")
-        S2(0, 0, 3, "PE")
-        e(2, 1, 1, "V")
-        e(2, 1, 2, "S")
-        f(2, 0, "V")
-        g(0, 0, 3, "V")
-        S2(0, 1, 2, "PE")
-        g(0, 1, 2, "V")
-        S2(0, 0, 0, "PE")
-        g(0, 0, 0, "V")
-        S2(0, 0, 2, "PE")
-        g(0, 0, 2, "V")
-        e(1, 1, 3, "S")
-        S2(0, 1, 3, "PE")
-        S2(0, 0, 1, "PE")
-        e(1, 0, 3, "S")
-        e(2, 1, 3, "S")
-        T(1, 1, 2, "PE")
-        T(1, 1, 1, "PE")
-        T(1, 0, 1, "PE")
+        d(0, 1, 0, "S")
+        d(1, 0, 3, "V")
+        d(0, 1, 1, "S")
+        S1(1, 1, 1, 2, "PE")
+        c(2, 0, 2, "V")
+        S1(1, 1, 0, 0, "PE")
+        S1(1, 1, 0, 1, "PE")
         T(1, 0, 0, "PE")
-        T(1, 0, 2, "PE")
-        e(1, 1, 2, "S")
-        S2(0, 1, 0, "PE")
-        g(0, 1, 3, "V")
-        f(2, 1, "V")
-        g(0, 0, 1, "V")
-        h(0, 0, 2, "V")
-        S2(0, 1, 1, "PE")
-        e(1, 1, 1, "S")
-        f(1, 1, "V")
-        S2(2, 0, 0, "PE")
-        e(1, 0, 1, "S")
-        h(0, 0, 0, "S")
-        e(1, 0, 2, "S")
-        g(0, 1, 0, "V")
-        g(0, 1, 1, "V")
+        c(0, 1, 2, "V")
+        T(0, 0, 0, "PE")
+        T(0, 1, 0, "PE")
+        d(0, 1, 3, "S")
+        c(2, 1, 3, "V")
+        d(2, 0, 3, "V")
+        d(0, 1, 2, "S")
         e(1, 0, 0, "S")
-        g(2, 0, 0, "V")
-        h(0, 0, 3, "S")
+        c(1, 1, 2, "V")
+        T(0, 0, 1, "PE")
+        T(1, 0, 1, "PE")
+        T(0, 1, 1, "PE")
+        e(0, 0, 1, "S")
+        S1(1, 1, 0, 2, "PE")
+        e(0, 0, 0, "V")
+        c(1, 1, 1, "V")
+        d(2, 0, 2, "V")
+        S1(2, 1, 0, 1, "PE")
+        S1(2, 1, 0, 2, "PE")
+        S1(1, 1, 3, 0, "PE")
+        f(0, 0, "V")
+        S1(2, 1, 2, 0, "PE")
+        e(0, 1, 1, "S")
+        S1(2, 1, 2, 1, "PE")
+        S1(1, 1, 3, 1, "PE")
+        c(1, 1, 0, "V")
+        S1(2, 1, 1, 0, "PE")
+        e(0, 1, 0, "S")
+        c(2, 1, 0, "V")
+        S1(2, 1, 2, 2, "PE")
+        d(1, 1, 2, "S")
+        S1(1, 1, 3, 2, "PE")
+        S1(2, 1, 1, 1, "PE")
+        f(0, 1, "V")
+        e(1, 0, 1, "S")
+        c(2, 1, 2, "V")
+        d(1, 1, 1, "S")
         f(1, 0, "V")
-        S2(2, 0, 1, "PE")
-        S2(2, 0, 2, "PE")
-        S2(2, 0, 3, "PE")
-        h(0, 0, 1, "S")
-        S2(1, 0, 3, "PE")
-        g(2, 0, 1, "V")
-        g(2, 0, 2, "V")
-        g(1, 0, 3, "V")
-        S2(1, 0, 2, "PE")
-        S2(1, 0, 1, "PE")
-        g(2, 0, 3, "V")
-        h(0, 1, 3, "S")
-        S2(2, 1, 2, "PE")
-        h(0, 1, 1, "S")
-        i(0, 0, "V")
+        c(1, 1, 3, "V")
+        d(2, 1, 0, "S")
+        d(2, 1, 3, "S")
+        S2(0, 1, 0, "PE")
+        S1(2, 1, 1, 2, "PE")
+        S2(0, 1, 3, "PE")
+        d(1, 1, 0, "S")
+        S2(0, 1, 1, "PE")
+        S2(0, 0, 0, "PE")
+        T(2, 0, 1, "PE")
+        d(2, 1, 2, "V")
+        d(1, 1, 3, "S")
+        c(2, 1, 1, "V")
+        g(0, 1, 0, "V")
+        d(2, 1, 1, "S")
+        e(2, 0, 1, "S")
+        T(2, 0, 0, "PE")
+        T(1, 1, 1, "PE")
+        g(0, 1, 3, "V")
+        S2(0, 1, 2, "PE")
+        g(0, 0, 0, "V")
+        e(1, 1, 1, "S")
+        T(1, 1, 0, "PE")
+        g(0, 1, 1, "V")
+        T(2, 1, 1, "PE")
+        g(0, 1, 2, "V")
+        e(2, 0, 0, "S")
+        f(2, 0, "V")
+        T(2, 1, 0, "PE")
+        e(1, 1, 0, "S")
+        S2(0, 0, 1, "PE")
+        S2(0, 0, 2, "PE")
+        f(1, 1, "V")
+        g(0, 0, 1, "V")
+        S2(0, 0, 3, "PE")
         h(0, 1, 0, "S")
+        e(2, 1, 1, "S")
         h(0, 1, 2, "S")
-        S2(1, 0, 0, "PE")
-        g(1, 0, 2, "V")
-        S2(2, 1, 3, "PE")
-        g(1, 0, 0, "V")
+        g(0, 0, 2, "V")
+        e(2, 1, 0, "S")
+        S2(1, 0, 1, "PE")
+        h(0, 1, 3, "S")
+        g(0, 0, 3, "V")
+        h(0, 0, 2, "S")
         g(1, 0, 1, "V")
-        g(2, 1, 2, "V")
-        S2(1, 1, 2, "PE")
-        i(0, 1, "V")
-        h(2, 0, 1, "S")
-        g(2, 1, 3, "V")
+        S2(1, 0, 2, "PE")
+        h(0, 1, 1, "S")
+        f(2, 1, "V")
+        S2(1, 0, 0, "PE")
         S2(1, 1, 1, "PE")
-        S2(2, 1, 1, "PE")
-        h(2, 0, 3, "S")
+        h(0, 0, 0, "S")
+        h(0, 0, 3, "S")
+        g(1, 0, 2, "V")
+        S2(1, 0, 3, "PE")
+        h(0, 0, 1, "S")
+        S2(2, 0, 1, "PE")
+        g(1, 0, 0, "V")
+        i(0, 1, "V")
+        S2(2, 0, 0, "PE")
+        g(1, 0, 3, "V")
+        S2(2, 0, 2, "PE")
+        S2(1, 1, 2, "PE")
+        h(1, 0, 1, "S")
+        g(2, 0, 0, "V")
         S2(2, 1, 0, "PE")
-        S2(1, 1, 3, "PE")
-        h(2, 0, 2, "S")
-        S3(1, 0, 0, "PE")
+        g(2, 0, 2, "V")
+        i(0, 0, "V")
+        S2(2, 0, 3, "PE")
+        g(2, 0, 1, "V")
         S2(1, 1, 0, "PE")
         S3(0, 0, 0, "PE")
-        h(2, 0, 0, "S")
-        g(2, 1, 0, "V")
-        g(1, 1, 1, "V")
-        S3(0, 2, 0, "PE")
-        S3(1, 3, 0, "PE")
-        h(1, 0, 0, "S")
-        g(1, 1, 3, "V")
-        h(1, 0, 1, "S")
-        h(1, 0, 2, "S")
-        S3(0, 3, 0, "PE")
-        h(1, 0, 3, "S")
-        g(2, 1, 1, "V")
-        h(2, 1, 0, "S")
-        i(1, 0, "V")
-        g(1, 1, 0, "V")
-        S3(0, 0, 1, "PE")
         S3(0, 1, 0, "PE")
-        S3(1, 1, 0, "PE")
+        h(1, 0, 2, "S")
+        h(1, 0, 3, "S")
+        g(2, 0, 3, "V")
+        h(1, 0, 0, "S")
+        h(2, 0, 1, "S")
+        S2(1, 1, 3, "PE")
+        S3(0, 3, 0, "PE")
+        g(1, 1, 1, "V")
         g(1, 1, 2, "V")
-        i(2, 0, "V")
-        S3(0, 2, 1, "PE")
-        S3(0, 1, 1, "PE")
-        S3(0, 1, 2, "PE")
-        S3(0, 3, 1, "PE")
-        h(2, 1, 1, "S")
-        h(1, 1, 3, "V")
-        h(2, 1, 3, "S")
-        h(1, 1, 0, "V")
-        S3(1, 2, 0, "PE")
+        h(2, 0, 3, "S")
+        g(1, 1, 3, "V")
+        S2(2, 1, 2, "PE")
+        g(1, 1, 0, "V")
+        i(1, 0, "V")
+        g(2, 1, 0, "V")
+        h(2, 0, 2, "S")
+        S2(2, 1, 3, "PE")
+        g(2, 1, 3, "V")
+        g(2, 1, 2, "V")
+        S2(2, 1, 1, "PE")
+        S3(0, 0, 1, "PE")
+        S3(1, 0, 0, "PE")
+        S3(1, 3, 0, "PE")
+        h(2, 0, 0, "S")
         h(1, 1, 1, "S")
-        S3(0, 0, 2, "PE")
-        S3(0, 3, 2, "PE")
+        S3(0, 2, 0, "PE")
+        g(2, 1, 1, "V")
+        S3(1, 2, 0, "PE")
+        i(2, 0, "V")
+        h(1, 1, 0, "S")
         h(1, 1, 2, "S")
-        j(0, 1, "V")
-        i(1, 1, "V")
-        j(0, 0, "V")
-        h(2, 1, 2, "S")
-        i(2, 1, "V")
+        h(1, 1, 3, "S")
+        S3(0, 1, 1, "PE")
+        S3(0, 2, 1, "PE")
+        S3(0, 1, 2, "PE")
         S3(0, 2, 2, "PE")
-        S3(1, 2, 1, "PE")
+        i(1, 1, "V")
+        S3(0, 0, 2, "PE")
+        h(2, 1, 3, "V")
+        h(2, 1, 0, "S")
+        S3(1, 1, 0, "PE")
+        j(0, 1, "V")
+        S3(0, 3, 1, "PE")
+        S3(0, 3, 2, "PE")
+        h(2, 1, 2, "S")
+        h(2, 1, 1, "S")
         S3(1, 3, 1, "PE")
-        j(0, 2, "V")
-        S3(1, 1, 1, "PE")
-        j(0, 3, "V")
+        j(0, 0, "V")
+        S3(1, 2, 1, "PE")
+        i(2, 1, "V")
         S3(1, 0, 1, "PE")
-        S3(1, 2, 2, "PE")
-        S3(1, 1, 2, "PE")
-        S3(1, 3, 2, "PE")
-        j(1, 2, "V")
-        j(1, 1, "V")
+        S3(1, 1, 1, "PE")
         S3(1, 0, 2, "PE")
-        j(1, 3, "V")
+        S3(1, 1, 2, "PE")
+        j(0, 2, "V")
+        j(0, 3, "V")
+        j(1, 1, "V")
+        S3(1, 3, 2, "PE")
+        S3(1, 2, 2, "PE")
+        j(1, 2, "V")
         j(1, 0, "V")
+        j(1, 3, "V")

@@ -82,9 +82,9 @@ def tile_household_bracket_response_t2_kernel(
             )
 
         load_x(0, 0)
+        load_x(1, 0)
         load_scales(a_sc, transfer_scales)
         load_a(0)
-        load_x(1, 0)
         load_x(2, 0)
         load_x(0, 1)
         load_a(1)
@@ -104,17 +104,16 @@ def tile_household_bracket_response_t2_kernel(
 
         a_w = [kt([P, HG, 2 * KP], U8, f"a_w_{g}") for g in range(HG)]
         a_s = [kt([P, HG, KP], U8, f"a_s_{g}") for g in range(HG)]
-        engines = {"V": nc.vector, "G": nc.gpsimd}
 
-        def k(g, t, e):
-            eng = engines[e]
-            eng.tensor_copy(
-                out=a_w[g][:, :, 2 * P * t : 2 * P * (t + 1)].rearrange("p k (m b) -> p k m b", b=2),
-                in_=a_nat[g][:].rearrange("p k (m t b) -> p k t m b", t=PACK, b=2)[:, :, t, :, :],
+        def k(g, q, e):
+            t0, t1 = 2 * q, 2 * q + 2
+            nc.vector.tensor_copy(
+                out=a_w[g][:].rearrange("p k (t m b) -> p t k m b", t=PACK, b=2)[:, t0:t1, :, :, :],
+                in_=a_nat[g][:].rearrange("p k (m t b) -> p t k m b", t=PACK, b=2)[:, t0:t1, :, :, :],
             )
-            eng.tensor_copy(
-                out=a_s[g][:, :, P * t : P * (t + 1)],
-                in_=a_sc[:, :, KP * g : KP * (g + 1)].rearrange("p k (m t) -> p k t m", t=PACK)[:, :, t, :],
+            nc.vector.tensor_copy(
+                out=a_s[g][:].rearrange("p k (t m) -> p t k m", t=PACK)[:, t0:t1, :, :],
+                in_=a_sc[:, :, KP * g : KP * (g + 1)].rearrange("p k (m t) -> p t k m", t=PACK)[:, t0:t1, :, :],
             )
 
         def interleave(e, out, in_):
@@ -136,7 +135,7 @@ def tile_household_bracket_response_t2_kernel(
 
         def a(g, hf, i, e):
             grouped = get(("xgr", g, hf), work, [P, N, PACK], BF16, "xgr", align_bytes=64, bufs=3)
-            cols = slice(P * i, P * (i + 1))
+            cols = slice(2 * P * i, 2 * P * (i + 1))
             interleave(e, grouped[:, cols, :], xt[g][hf][:, :, cols].rearrange("p t c -> p c t"))
 
         def b(g, hf, e):
@@ -248,7 +247,7 @@ def tile_household_bracket_response_t2_kernel(
 
         def h(g, hf, i, e):
             grouped = get(("x2gr", g, hf), work, [P, N, PACK], BF16, "x2gr", align_bytes=64, bufs=2)
-            cols = slice(P * i, P * (i + 1))
+            cols = slice(2 * P * i, 2 * P * (i + 1))
             interleave(e, grouped[:, cols, :], made[("x2", g, hf)][:, :, cols].rearrange("p t c -> p c t"))
 
         def i(g, hf, e):
@@ -282,305 +281,275 @@ def tile_household_bracket_response_t2_kernel(
             nc.sync.dma_start(out=out[P * j : P * (j + 1), N * hf : N * (hf + 1)], in_=o[:])
 
         ctx.enter_context(tc.manual_schedule())
-        a(1, 0, 2, "S")
-        a(1, 0, 0, "S")
-        a(0, 0, 0, "V")
-        a(1, 0, 3, "S")
-        a(0, 0, 3, "V")
         a(0, 0, 1, "V")
-        a(0, 0, 2, "V")
+        a(0, 0, 0, "S")
+        a(1, 0, 1, "S")
+        a(1, 0, 0, "V")
         b(0, 0, "V")
-        k(0, 1, "V")
-        S1(0, 0, 1, 0, "PE")
-        k(0, 3, "V")
-        k(0, 2, "V")
-        S1(0, 0, 2, 0, "PE")
-        a(1, 0, 1, "V")
-        k(0, 0, "V")
-        a(2, 0, 3, "S")
-        S1(0, 0, 0, 0, "PE")
         b(1, 0, "V")
-        S1(0, 0, 3, 0, "PE")
-        k(1, 0, "V")
-        S1(1, 0, 0, 0, "PE")
+        k(0, 0, "V")
+        a(2, 0, 1, "V")
+        S1(0, 0, 1, 0, "PE")
+        k(0, 1, "V")
         a(2, 0, 0, "S")
-        S1(0, 0, 2, 1, "PE")
-        S1(0, 0, 0, 1, "PE")
-        k(1, 2, "V")
-        S1(0, 0, 1, 1, "PE")
-        k(1, 1, "V")
-        a(2, 0, 2, "S")
-        S1(1, 0, 2, 0, "PE")
-        a(2, 0, 1, "S")
-        a(1, 1, 1, "S")
-        a(1, 1, 0, "S")
-        S1(1, 0, 2, 1, "PE")
-        k(1, 3, "V")
-        a(0, 1, 3, "S")
-        b(2, 0, "V")
-        S1(1, 0, 3, 0, "PE")
-        S1(1, 0, 0, 1, "PE")
-        S1(0, 0, 3, 1, "PE")
-        S1(0, 0, 3, 2, "PE")
-        S1(0, 0, 0, 2, "PE")
-        k(2, 1, "V")
-        k(2, 3, "V")
-        a(0, 1, 1, "S")
-        c(0, 0, 0, "V")
-        S1(2, 0, 1, 0, "PE")
-        S1(2, 0, 1, 1, "PE")
         a(0, 1, 0, "S")
-        S1(0, 0, 2, 2, "PE")
-        a(2, 1, 1, "S")
-        S1(1, 0, 3, 1, "PE")
-        k(2, 0, "V")
-        S1(2, 0, 1, 2, "PE")
-        c(0, 0, 2, "V")
-        c(2, 0, 1, "V")
-        a(1, 1, 2, "S")
-        a(0, 1, 2, "S")
-        S1(1, 0, 3, 2, "PE")
-        a(2, 1, 2, "S")
-        S1(0, 0, 1, 2, "PE")
-        a(1, 1, 3, "S")
-        k(2, 2, "V")
-        S1(1, 0, 1, 0, "PE")
-        d(0, 0, 2, "S")
-        S1(1, 0, 1, 1, "PE")
-        c(1, 0, 3, "V")
-        b(0, 1, "V")
-        S1(2, 0, 0, 0, "PE")
-        d(0, 0, 0, "S")
-        S1(1, 0, 1, 2, "PE")
-        c(1, 0, 1, "V")
-        a(2, 1, 3, "S")
-        S1(2, 0, 3, 0, "PE")
-        d(1, 0, 1, "S")
-        S1(2, 0, 3, 1, "PE")
-        S1(1, 0, 2, 2, "PE")
-        S1(2, 0, 2, 0, "PE")
+        S1(0, 0, 3, 0, "PE")
+        S1(0, 0, 2, 0, "PE")
+        S1(0, 0, 3, 1, "PE")
+        a(0, 1, 1, "S")
+        b(2, 0, "V")
+        a(1, 1, 0, "S")
+        S1(0, 0, 3, 2, "PE")
+        k(1, 1, "V")
+        S1(0, 0, 1, 1, "PE")
+        k(1, 0, "V")
+        S1(0, 0, 0, 0, "PE")
+        a(1, 1, 1, "S")
         a(2, 1, 0, "S")
-        S1(2, 0, 3, 2, "PE")
-        b(1, 1, "V")
-        c(1, 0, 2, "V")
-        S1(2, 0, 2, 1, "PE")
-        S1(2, 0, 0, 1, "PE")
-        S1(2, 0, 2, 2, "PE")
-        S1(1, 0, 0, 2, "PE")
-        d(1, 0, 2, "S")
-        S1(2, 0, 0, 2, "PE")
-        c(1, 0, 0, "V")
-        S1(0, 1, 0, 0, "PE")
-        c(2, 0, 0, "V")
-        S1(0, 1, 0, 1, "PE")
-        S1(0, 1, 3, 0, "PE")
-        S1(0, 1, 3, 1, "PE")
-        S1(2, 1, 3, 0, "PE")
-        S1(0, 1, 2, 0, "PE")
-        b(2, 1, "V")
-        S1(0, 1, 2, 1, "PE")
-        d(2, 0, 1, "S")
+        S1(0, 0, 2, 1, "PE")
+        S1(1, 0, 2, 0, "PE")
+        S1(1, 0, 2, 1, "PE")
+        S1(1, 0, 2, 2, "PE")
+        S1(0, 0, 1, 2, "PE")
+        a(2, 1, 1, "S")
+        S1(0, 0, 0, 1, "PE")
+        S1(0, 0, 0, 2, "PE")
+        S1(1, 0, 3, 0, "PE")
+        S1(1, 0, 1, 0, "PE")
+        S1(1, 0, 1, 1, "PE")
+        S1(1, 0, 1, 2, "PE")
+        b(0, 1, "V")
         c(0, 0, 1, "V")
-        S1(2, 1, 3, 1, "PE")
-        S1(0, 1, 3, 2, "PE")
-        S1(0, 1, 0, 2, "PE")
         c(0, 0, 3, "V")
-        d(2, 0, 0, "S")
-        c(2, 0, 3, "V")
-        d(0, 0, 1, "S")
-        c(0, 1, 0, "V")
-        S1(1, 1, 1, 0, "PE")
-        S1(1, 1, 1, 1, "PE")
-        d(0, 0, 3, "S")
-        c(0, 1, 3, "V")
-        S1(0, 1, 1, 0, "PE")
+        S1(1, 0, 0, 0, "PE")
+        S1(1, 0, 0, 1, "PE")
+        c(1, 0, 2, "V")
+        S1(1, 0, 3, 1, "PE")
         S1(1, 1, 2, 0, "PE")
+        S1(0, 1, 1, 0, "PE")
+        b(1, 1, "V")
+        c(0, 0, 0, "V")
+        S1(1, 0, 3, 2, "PE")
+        d(0, 0, 1, "S")
+        S1(0, 1, 0, 0, "PE")
         S1(0, 1, 1, 1, "PE")
-        S1(0, 1, 1, 2, "PE")
-        S1(0, 1, 2, 2, "PE")
-        c(0, 1, 1, "V")
+        d(0, 0, 0, "S")
+        S1(0, 1, 0, 1, "PE")
+        c(1, 0, 1, "V")
+        c(1, 0, 3, "V")
+        S1(0, 0, 2, 2, "PE")
+        c(0, 0, 2, "V")
+        S1(0, 1, 3, 0, "PE")
+        S1(1, 0, 0, 2, "PE")
+        S1(0, 1, 3, 1, "PE")
+        d(0, 0, 3, "S")
+        c(1, 0, 0, "V")
+        d(0, 0, 2, "S")
+        S1(0, 1, 2, 0, "PE")
+        S1(1, 1, 3, 0, "PE")
+        b(2, 1, "V")
         S1(1, 1, 2, 1, "PE")
-        S1(2, 1, 0, 0, "PE")
-        d(1, 0, 0, "S")
+        S1(0, 1, 2, 1, "PE")
+        T(0, 0, 0, "PE")
+        k(2, 0, "V")
+        e(0, 0, 0, "S")
+        T(0, 0, 1, "PE")
+        S1(0, 1, 3, 2, "PE")
+        S1(1, 1, 3, 1, "PE")
+        S1(1, 1, 3, 2, "PE")
+        S1(0, 1, 1, 2, "PE")
+        c(0, 1, 3, "V")
+        S1(0, 1, 2, 2, "PE")
+        S1(0, 1, 0, 2, "PE")
+        k(2, 1, "V")
+        d(1, 0, 2, "S")
+        S1(2, 1, 1, 0, "PE")
+        c(0, 1, 2, "V")
+        e(0, 0, 1, "S")
+        S1(2, 0, 1, 0, "PE")
+        S1(2, 1, 1, 1, "PE")
         S1(1, 1, 2, 2, "PE")
-        S1(2, 1, 3, 2, "PE")
-        d(0, 1, 0, "S")
-        d(1, 0, 3, "V")
-        d(0, 1, 1, "S")
-        S1(1, 1, 1, 2, "PE")
-        c(2, 0, 2, "V")
+        c(0, 1, 0, "V")
+        S1(2, 0, 1, 1, "PE")
+        S1(2, 1, 1, 2, "PE")
+        S1(2, 0, 1, 2, "PE")
+        c(1, 1, 3, "V")
+        S1(2, 0, 2, 0, "PE")
+        c(0, 1, 1, "V")
+        S1(1, 1, 1, 0, "PE")
+        c(1, 1, 2, "V")
+        S1(2, 0, 0, 0, "PE")
+        S1(1, 1, 1, 1, "PE")
+        d(1, 0, 1, "S")
+        d(1, 0, 0, "S")
         S1(1, 1, 0, 0, "PE")
         S1(1, 1, 0, 1, "PE")
-        T(1, 0, 0, "PE")
-        c(0, 1, 2, "V")
-        T(0, 0, 0, "PE")
-        T(0, 1, 0, "PE")
+        d(1, 0, 3, "S")
+        d(0, 1, 0, "S")
         d(0, 1, 3, "S")
-        c(2, 1, 3, "V")
-        d(2, 0, 3, "V")
-        d(0, 1, 2, "S")
-        e(1, 0, 0, "S")
-        c(1, 1, 2, "V")
-        T(0, 0, 1, "PE")
-        T(1, 0, 1, "PE")
-        T(0, 1, 1, "PE")
-        e(0, 0, 1, "S")
         S1(1, 1, 0, 2, "PE")
-        e(0, 0, 0, "V")
-        c(1, 1, 1, "V")
-        d(2, 0, 2, "V")
-        S1(2, 1, 0, 1, "PE")
-        S1(2, 1, 0, 2, "PE")
-        S1(1, 1, 3, 0, "PE")
-        f(0, 0, "V")
-        S1(2, 1, 2, 0, "PE")
-        e(0, 1, 1, "S")
-        S1(2, 1, 2, 1, "PE")
-        S1(1, 1, 3, 1, "PE")
-        c(1, 1, 0, "V")
-        S1(2, 1, 1, 0, "PE")
-        e(0, 1, 0, "S")
-        c(2, 1, 0, "V")
-        S1(2, 1, 2, 2, "PE")
-        d(1, 1, 2, "S")
-        S1(1, 1, 3, 2, "PE")
-        S1(2, 1, 1, 1, "PE")
-        f(0, 1, "V")
-        e(1, 0, 1, "S")
-        c(2, 1, 2, "V")
-        d(1, 1, 1, "S")
-        f(1, 0, "V")
-        c(1, 1, 3, "V")
-        d(2, 1, 0, "S")
-        d(2, 1, 3, "S")
-        S2(0, 1, 0, "PE")
-        S1(2, 1, 1, 2, "PE")
-        S2(0, 1, 3, "PE")
-        d(1, 1, 0, "S")
-        S2(0, 1, 1, "PE")
-        S2(0, 0, 0, "PE")
-        T(2, 0, 1, "PE")
-        d(2, 1, 2, "V")
+        S1(2, 1, 3, 0, "PE")
+        S1(2, 0, 2, 1, "PE")
         d(1, 1, 3, "S")
+        S1(1, 1, 1, 2, "PE")
+        d(0, 1, 2, "S")
+        c(1, 1, 0, "V")
+        d(1, 1, 0, "S")
         c(2, 1, 1, "V")
-        g(0, 1, 0, "V")
-        d(2, 1, 1, "S")
-        e(2, 0, 1, "S")
-        T(2, 0, 0, "PE")
+        S1(2, 0, 2, 2, "PE")
+        S1(2, 1, 3, 1, "PE")
+        c(2, 0, 2, "V")
+        c(1, 1, 1, "V")
+        S1(2, 1, 3, 2, "PE")
+        S1(2, 1, 0, 0, "PE")
+        S1(2, 1, 0, 1, "PE")
+        S1(2, 0, 0, 1, "PE")
+        f(0, 0, "V")
+        S1(2, 0, 0, 2, "PE")
+        S1(2, 1, 0, 2, "PE")
+        T(1, 0, 0, "PE")
+        T(0, 1, 1, "PE")
+        d(0, 1, 1, "S")
+        d(1, 1, 2, "S")
+        d(2, 0, 2, "S")
+        d(1, 1, 1, "S")
+        T(0, 1, 0, "PE")
+        T(1, 0, 1, "PE")
+        c(2, 1, 0, "V")
+        e(0, 1, 1, "S")
         T(1, 1, 1, "PE")
-        g(0, 1, 3, "V")
-        S2(0, 1, 2, "PE")
-        g(0, 0, 0, "V")
-        e(1, 1, 1, "S")
-        T(1, 1, 0, "PE")
-        g(0, 1, 1, "V")
-        T(2, 1, 1, "PE")
-        g(0, 1, 2, "V")
-        e(2, 0, 0, "S")
-        f(2, 0, "V")
-        T(2, 1, 0, "PE")
-        e(1, 1, 0, "S")
-        S2(0, 0, 1, "PE")
-        S2(0, 0, 2, "PE")
-        f(1, 1, "V")
-        g(0, 0, 1, "V")
+        e(0, 1, 0, "S")
+        S1(2, 1, 2, 0, "PE")
+        c(2, 1, 3, "V")
+        c(2, 0, 1, "V")
+        S1(2, 1, 2, 1, "PE")
+        c(2, 0, 0, "V")
+        S1(2, 1, 2, 2, "PE")
+        S1(2, 0, 3, 0, "PE")
+        e(1, 0, 0, "S")
+        f(0, 1, "V")
+        S1(2, 0, 3, 1, "PE")
+        S1(2, 0, 3, 2, "PE")
         S2(0, 0, 3, "PE")
-        h(0, 1, 0, "S")
-        e(2, 1, 1, "S")
-        h(0, 1, 2, "S")
-        g(0, 0, 2, "V")
-        e(2, 1, 0, "S")
-        S2(1, 0, 1, "PE")
-        h(0, 1, 3, "S")
+        c(2, 1, 2, "V")
+        d(2, 0, 1, "S")
+        d(2, 1, 3, "S")
+        d(2, 0, 0, "S")
+        c(2, 0, 3, "V")
+        S2(0, 1, 2, "PE")
+        S2(0, 0, 2, "PE")
+        e(1, 0, 1, "S")
         g(0, 0, 3, "V")
-        h(0, 0, 2, "S")
-        g(1, 0, 1, "V")
-        S2(1, 0, 2, "PE")
-        h(0, 1, 1, "S")
-        f(2, 1, "V")
+        g(0, 1, 2, "V")
+        S2(0, 1, 3, "PE")
+        d(2, 1, 2, "S")
+        f(1, 0, "V")
+        g(0, 1, 3, "V")
+        e(1, 1, 1, "S")
+        d(2, 0, 3, "S")
+        T(1, 1, 0, "PE")
+        d(2, 1, 1, "S")
+        g(0, 0, 2, "V")
+        S2(0, 0, 1, "PE")
+        e(1, 1, 0, "S")
+        S2(0, 0, 0, "PE")
+        S2(0, 1, 0, "PE")
+        g(0, 0, 1, "V")
+        d(2, 1, 0, "S")
+        T(2, 0, 0, "PE")
+        e(2, 0, 0, "S")
+        f(1, 1, "V")
+        T(2, 0, 1, "PE")
+        g(0, 0, 0, "V")
+        e(2, 0, 1, "S")
+        T(2, 1, 1, "PE")
+        S2(0, 1, 1, "PE")
+        T(2, 1, 0, "PE")
+        g(0, 1, 0, "V")
+        S2(1, 0, 1, "PE")
+        e(2, 1, 1, "S")
+        e(2, 1, 0, "S")
+        f(2, 0, "V")
         S2(1, 0, 0, "PE")
-        S2(1, 1, 1, "PE")
-        h(0, 0, 0, "S")
-        h(0, 0, 3, "S")
-        g(1, 0, 2, "V")
+        g(0, 1, 1, "V")
+        f(2, 1, "V")
+        g(1, 0, 1, "V")
         S2(1, 0, 3, "PE")
-        h(0, 0, 1, "S")
-        S2(2, 0, 1, "PE")
+        S2(1, 1, 1, "PE")
         g(1, 0, 0, "V")
-        i(0, 1, "V")
-        S2(2, 0, 0, "PE")
+        S2(1, 0, 2, "PE")
+        h(0, 0, 1, "S")
+        h(0, 0, 0, "S")
+        S2(2, 0, 3, "PE")
+        h(0, 1, 1, "S")
+        h(0, 1, 0, "S")
         g(1, 0, 3, "V")
-        S2(2, 0, 2, "PE")
-        S2(1, 1, 2, "PE")
-        h(1, 0, 1, "S")
+        g(1, 0, 2, "V")
+        g(2, 0, 3, "V")
+        S2(2, 0, 1, "PE")
+        g(2, 0, 1, "V")
+        S2(2, 0, 0, "PE")
+        i(0, 0, "V")
         g(2, 0, 0, "V")
         S2(2, 1, 0, "PE")
-        g(2, 0, 2, "V")
-        i(0, 0, "V")
-        S2(2, 0, 3, "PE")
-        g(2, 0, 1, "V")
-        S2(1, 1, 0, "PE")
-        S3(0, 0, 0, "PE")
-        S3(0, 1, 0, "PE")
-        h(1, 0, 2, "S")
-        h(1, 0, 3, "S")
-        g(2, 0, 3, "V")
-        h(1, 0, 0, "S")
-        h(2, 0, 1, "S")
         S2(1, 1, 3, "PE")
-        S3(0, 3, 0, "PE")
-        g(1, 1, 1, "V")
-        g(1, 1, 2, "V")
-        h(2, 0, 3, "S")
         g(1, 1, 3, "V")
-        S2(2, 1, 2, "PE")
-        g(1, 1, 0, "V")
-        i(1, 0, "V")
-        g(2, 1, 0, "V")
-        h(2, 0, 2, "S")
-        S2(2, 1, 3, "PE")
-        g(2, 1, 3, "V")
-        g(2, 1, 2, "V")
-        S2(2, 1, 1, "PE")
-        S3(0, 0, 1, "PE")
-        S3(1, 0, 0, "PE")
-        S3(1, 3, 0, "PE")
-        h(2, 0, 0, "S")
-        h(1, 1, 1, "S")
+        S2(2, 0, 2, "PE")
         S3(0, 2, 0, "PE")
-        g(2, 1, 1, "V")
-        S3(1, 2, 0, "PE")
-        i(2, 0, "V")
-        h(1, 1, 0, "S")
-        h(1, 1, 2, "S")
-        h(1, 1, 3, "S")
+        S2(2, 1, 2, "PE")
+        i(0, 1, "V")
+        h(1, 0, 1, "S")
+        S2(1, 1, 0, "PE")
+        g(2, 0, 2, "V")
+        S2(1, 1, 2, "PE")
+        g(1, 1, 0, "V")
+        S3(0, 1, 0, "PE")
+        S3(1, 0, 0, "PE")
+        h(1, 0, 0, "S")
+        g(1, 1, 1, "V")
+        i(1, 0, "V")
+        g(2, 1, 2, "V")
+        S3(0, 0, 0, "PE")
+        g(1, 1, 2, "V")
+        S2(2, 1, 1, "PE")
+        h(2, 0, 1, "S")
+        h(2, 0, 0, "S")
+        S3(0, 3, 0, "PE")
         S3(0, 1, 1, "PE")
-        S3(0, 2, 1, "PE")
-        S3(0, 1, 2, "PE")
-        S3(0, 2, 2, "PE")
-        i(1, 1, "V")
+        g(2, 1, 1, "V")
+        S3(0, 0, 1, "PE")
+        S2(2, 1, 3, "PE")
+        i(2, 0, "V")
         S3(0, 0, 2, "PE")
-        h(2, 1, 3, "V")
+        g(2, 1, 0, "V")
+        h(1, 1, 0, "S")
+        S3(0, 1, 2, "PE")
+        S3(0, 2, 1, "PE")
+        S3(1, 2, 0, "PE")
+        g(2, 1, 3, "V")
+        S3(0, 2, 2, "PE")
+        h(1, 1, 1, "S")
+        S3(1, 3, 0, "PE")
         h(2, 1, 0, "S")
-        S3(1, 1, 0, "PE")
-        j(0, 1, "V")
-        S3(0, 3, 1, "PE")
-        S3(0, 3, 2, "PE")
-        h(2, 1, 2, "S")
-        h(2, 1, 1, "S")
-        S3(1, 3, 1, "PE")
         j(0, 0, "V")
-        S3(1, 2, 1, "PE")
+        h(2, 1, 1, "V")
+        i(1, 1, "V")
         i(2, 1, "V")
-        S3(1, 0, 1, "PE")
-        S3(1, 1, 1, "PE")
-        S3(1, 0, 2, "PE")
-        S3(1, 1, 2, "PE")
-        j(0, 2, "V")
+        S3(0, 3, 1, "PE")
+        j(0, 1, "V")
+        S3(0, 3, 2, "PE")
+        S3(1, 1, 0, "PE")
         j(0, 3, "V")
-        j(1, 1, "V")
-        S3(1, 3, 2, "PE")
+        S3(1, 2, 1, "PE")
+        S3(1, 3, 1, "PE")
+        S3(1, 0, 1, "PE")
+        j(0, 2, "V")
+        S3(1, 0, 2, "PE")
         S3(1, 2, 2, "PE")
         j(1, 2, "V")
         j(1, 0, "V")
+        S3(1, 3, 2, "PE")
+        S3(1, 1, 1, "PE")
         j(1, 3, "V")
+        S3(1, 1, 2, "PE")
+        j(1, 1, "V")

@@ -4,6 +4,7 @@ import concourse.mybir as mybir
 from concourse.masks import make_identity
 
 H, C, G = 1536, 1024, 512
+FLOPS = 2 * (H * H * C + H * C * C + H * G * C)
 
 F32 = mybir.dt.float32
 BF16 = mybir.dt.bfloat16
@@ -15,14 +16,16 @@ FP4X4 = mybir.dt.float4_e2m1fn_x4
 ADD = mybir.AluOpType.add
 MULT = mybir.AluOpType.mult
 
-FLOPS = 2 * (H * H * C + H * C * C + H * G * C)
-
 P = 128
 PACK = 4
-KP = P * PACK
-HG = H // KP
-CG = C // KP
-N = 512
+K_PASS = P * PACK
+GROUPS = H // K_PASS
+HALVES = C // K_PASS
+HALF = K_PASS
+PART = HALF // 2
+OUT_TILES = G // P
+BANKS = 8
+E2M1_BYTES = 2
 
 
 def tile_household_bracket_response_t2_kernel(
@@ -43,513 +46,403 @@ def tile_household_bracket_response_t2_kernel(
         keep = ctx.enter_context(tc.tile_pool(name="keep", bufs=1))
         work = ctx.enter_context(tc.tile_pool(name="work", bufs=3))
         psum = ctx.enter_context(tc.psum_pool(name="psum", bufs=1))
-        free_banks = list(range(8))
+        ctx.enter_context(tc.manual_schedule())
 
-        def kt(shape, dtype, name):
+        def kept(shape, dtype, name):
             return keep.tile(shape, dtype, name=name, align_bytes=64)
 
-        a_sc = kt([P, HG, H], U8, "a_sc")
-        r_sc = kt([P, CG, C], U8, "r_sc")
-        b_sc = kt([P, HG, G], U8, "b_sc")
-        nc.vector.memset(a_sc[:].bitcast(I32), 0)
-        nc.gpsimd.memset(r_sc[:].bitcast(I32), 0)
-        nc.gpsimd.memset(b_sc[:].bitcast(I32), 0)
-        ident = kt([P, P], F32, "ident")
-        make_identity(nc, ident[:])
+        a_scales_in = [kept([P, GROUPS, K_PASS], U8, "a_scales_first"), kept([P, GROUPS, H - K_PASS], U8, "a_scales_rest")]
+        r_scales = kept([P, HALVES, C], U8, "r_scales")
+        b_scales = kept([P, GROUPS, G], U8, "b_scales")
+        nc.vector.memset(a_scales_in[0][:].bitcast(I32), 0)
+        nc.gpsimd.memset(a_scales_in[1][:].bitcast(I32), 0)
+        nc.gpsimd.memset(r_scales[:].bitcast(I32), 0)
+        nc.gpsimd.memset(b_scales[:].bitcast(I32), 0)
+        identity = kept([P, P], F32, "identity")
+        make_identity(nc, identity[:])
 
-        def load_scales(tile, dram):
-            view = tile[:].bitcast(I32)
+        def load_scales(plane, scales):
+            words = plane[:].bitcast(I32)
             for q in range(4):
                 nc.sync.dma_start(
-                    out=view[32 * q : 32 * q + 4, :, :],
-                    in_=dram[:, 4 * q : 4 * q + 4, :].rearrange("k r n -> r k n").bitcast(I32),
+                    out=words[32 * q : 32 * q + 4, :, :],
+                    in_=scales[:, 4 * q : 4 * q + 4, :].rearrange("k r n -> r k n").bitcast(I32),
                 )
 
-        xt = [[kt([P, PACK, N], BF16, f"x_{g}_{hf}") for hf in range(2)] for g in range(HG)]
+        def load_words(tile, words):
+            nc.sync.dma_start(out=tile[:].bitcast(I32), in_=words.rearrange("k p n -> p k n").bitcast(I32))
 
-        def load_x(g, hf):
+        x_in = [[kept([P, PACK, HALF], BF16, f"x_{g}_{half}") for half in range(HALVES)] for g in range(GROUPS)]
+        a_in = [kept([P, GROUPS, E2M1_BYTES * K_PASS], U8, f"a_in_{g}") for g in range(GROUPS)]
+        r_words = kept([P, HALVES, E2M1_BYTES * C], U8, "r_words")
+        b_words = kept([P, GROUPS, E2M1_BYTES * G], U8, "b_words")
+        prop = kept([P, GROUPS, PACK], BF16, "prop")
+        rates = kept([P, OUT_TILES, C], BF16, "rates")
+
+        def load_x(g, half):
             nc.sync.dma_start(
-                out=xt[g][hf][:],
-                in_=x[KP * g : KP * (g + 1), N * hf : N * (hf + 1)].rearrange("(p t) c -> p t c", t=PACK),
+                out=x_in[g][half][:],
+                in_=x[K_PASS * g : K_PASS * (g + 1), HALF * half : HALF * (half + 1)].rearrange("(p t) c -> p t c", t=PACK),
             )
-
-        a_nat = [kt([P, HG, 2 * KP], U8, f"a_nat_{g}") for g in range(HG)]
 
         def load_a(g):
-            nc.sync.dma_start(
-                out=a_nat[g][:].bitcast(I32),
-                in_=transfer_words[:, :, 2 * KP * g : 2 * KP * (g + 1)].rearrange("k p n -> p k n").bitcast(I32),
-            )
+            width = E2M1_BYTES * K_PASS
+            load_words(a_in[g], transfer_words[:, :, width * g : width * (g + 1)])
 
+        load_a(0)
+        load_scales(a_scales_in[0], transfer_scales[:, :, :K_PASS])
         load_x(0, 0)
         load_x(1, 0)
-        load_scales(a_sc, transfer_scales)
-        load_a(0)
         load_x(2, 0)
         load_x(0, 1)
+        load_scales(a_scales_in[1], transfer_scales[:, :, K_PASS:])
         load_a(1)
         load_x(1, 1)
         load_x(2, 1)
         load_a(2)
-        load_scales(r_sc, reclass_scales)
-        r_w = kt([P, CG, 2 * C], U8, "r_w")
-        nc.sync.dma_start(out=r_w[:].bitcast(I32), in_=reclass_words.rearrange("k p n -> p k n").bitcast(I32))
-        prop = kt([P, HG, PACK], BF16, "prop")
+        load_scales(r_scales, reclass_scales)
+        load_words(r_words, reclass_words)
         nc.sync.dma_start(out=prop[:], in_=propensity.rearrange("(g p t) -> p g t", p=P, t=PACK))
-        load_scales(b_sc, bracket_scales)
-        b_w = kt([P, HG, 2 * G], U8, "b_w")
-        nc.sync.dma_start(out=b_w[:].bitcast(I32), in_=bracket_words.rearrange("k p n -> p k n").bitcast(I32))
-        rate_t = kt([P, 4, C], BF16, "rate_t")
-        nc.sync.dma_start(out=rate_t[:], in_=rate.rearrange("(j p) c -> p j c", p=P))
+        load_scales(b_scales, bracket_scales)
+        load_words(b_words, bracket_words)
+        nc.sync.dma_start(out=rates[:], in_=rate.rearrange("(j p) c -> p j c", p=P))
 
-        a_w = [kt([P, HG, 2 * KP], U8, f"a_w_{g}") for g in range(HG)]
-        a_s = [kt([P, HG, KP], U8, f"a_s_{g}") for g in range(HG)]
-
-        def k(g, q, e):
-            t0, t1 = 2 * q, 2 * q + 2
-            nc.vector.tensor_copy(
-                out=a_w[g][:].rearrange("p k (t m b) -> p t k m b", t=PACK, b=2)[:, t0:t1, :, :, :],
-                in_=a_nat[g][:].rearrange("p k (m t b) -> p t k m b", t=PACK, b=2)[:, t0:t1, :, :, :],
-            )
-            nc.vector.tensor_copy(
-                out=a_s[g][:].rearrange("p k (t m) -> p t k m", t=PACK)[:, t0:t1, :, :],
-                in_=a_sc[:, :, KP * g : KP * (g + 1)].rearrange("p k (m t) -> p t k m", t=PACK)[:, t0:t1, :, :],
-            )
-
-        def interleave(e, out, in_):
-            if e == "V":
-                nc.vector.tensor_copy(out=out, in_=in_)
-            elif e == "S":
-                nc.scalar.copy(out=out, in_=in_)
-            else:
-                nc.gpsimd.tensor_scalar(out=out, in0=in_, scalar1=1.0, scalar2=0.0, op0=MULT, op1=ADD)
-
-        xq = [kt([P, C], U32, f"xq_{g}") for g in range(HG)]
-        xs = [kt([P, C], U8, f"xs_{g}") for g in range(HG)]
-        made = {}
-
-        def get(key, pool, shape, dtype, name, **kw):
-            if key not in made:
-                made[key] = pool.tile(shape, dtype, name=name, **kw)
-            return made[key]
-
-        def a(g, hf, i, e):
-            grouped = get(("xgr", g, hf), work, [P, N, PACK], BF16, "xgr", align_bytes=64, bufs=3)
-            cols = slice(2 * P * i, 2 * P * (i + 1))
-            interleave(e, grouped[:, cols, :], xt[g][hf][:, :, cols].rearrange("p t c -> p c t"))
-
-        def b(g, hf, e):
-            nc.vector.quantize_mx(
-                out=xq[g][:, N * hf : N * (hf + 1)].bitcast(FP8X4),
-                scales=xs[g][:, N * hf : N * (hf + 1)],
-                in_=made[("xgr", g, hf)][:].rearrange("p c t -> p (c t)"),
-            )
-
-        banks = {}
+        closed_banks = list(range(BANKS))
+        open_banks = {}
 
         def open_bank(key, shape):
-            n = free_banks.pop(0)
-            tile = psum.tile(shape, F32, name="bank", tag=f"bank{n}")
-            banks[key] = tile, n
+            bank = closed_banks.pop(0)
+            tile = psum.tile(shape, F32, name="acc", tag=f"bank_{bank}")
+            open_banks[key] = bank, tile
             return tile
 
         def close_bank(key):
-            tile, n = banks[key]
-            free_banks.append(n)
+            bank, tile = open_banks.pop(key)
+            closed_banks.append(bank)
             return tile
 
-        x1 = [kt([P, PACK, C], F32, f"x1_{g}") for g in range(HG)]
+        staged = {}
 
-        def S1(g, hf, t, kk, e):
-            if kk == 0:
-                open_bank((g, hf, t), [P, N])
-            nc.tensor.matmul_mx(
-                out=banks[(g, hf, t)][0][:],
-                lhsT=a_w[g][:, kk, 2 * P * t : 2 * P * (t + 1)].bitcast(FP4X4),
-                lhsT_scale=a_s[g][:, kk, P * t : P * (t + 1)],
-                rhs=xq[kk][:, N * hf : N * (hf + 1)].bitcast(FP8X4),
-                rhs_scale=xs[kk][:, N * hf : N * (hf + 1)],
-                start=(kk == 0),
-                stop=(kk == HG - 1),
+        def stage(kind, key, shape, bufs):
+            if (kind, key) not in staged:
+                tile = work.tile(shape, BF16, name=kind, tag=kind, bufs=bufs, align_bytes=64)
+                staged[kind, key] = tile
+            return staged[kind, key]
+
+        def copy(engine, out_ap, in_ap):
+            if engine == "vector":
+                nc.vector.tensor_copy(out=out_ap, in_=in_ap)
+            else:
+                nc.scalar.copy(out=out_ap, in_=in_ap)
+
+        def flat(tile):
+            return tile[:].rearrange("p c t -> p (c t)")
+
+        a_words = [kept([P, GROUPS, E2M1_BYTES * K_PASS], U8, f"a_words_{g}") for g in range(GROUPS)]
+        a_scales = [kept([P, GROUPS, K_PASS], U8, f"a_scales_{g}") for g in range(GROUPS)]
+
+        def reorder_a_words(g, pair):
+            tiles = slice(2 * pair, 2 * pair + 2)
+            nc.vector.tensor_copy(
+                out=a_words[g][:].rearrange("p k (t m b) -> p t k m b", t=PACK, b=E2M1_BYTES)[:, tiles, :, :, :],
+                in_=a_in[g][:].rearrange("p k (m t b) -> p t k m b", t=PACK, b=E2M1_BYTES)[:, tiles, :, :, :],
             )
 
-        x1q = [[kt([P, KP], U32, f"x1q_{g}_{hf}") for hf in range(2)] for g in range(HG)]
-        x1s = [[kt([P, KP], U8, f"x1s_{g}_{hf}") for hf in range(2)] for g in range(HG)]
-
-        def c(g, hf, t, e):
-            nc.vector.tensor_tensor(
-                out=x1[g][:, t, N * hf : N * (hf + 1)],
-                in0=close_bank((g, hf, t))[:],
-                in1=xt[g][hf][:, t, :],
-                op=ADD,
+        def reorder_a_scales(g):
+            if g == 0:
+                scales_in = a_scales_in[0][:]
+            else:
+                scales_in = a_scales_in[1][:, :, K_PASS * (g - 1) : K_PASS * g]
+            nc.vector.tensor_copy(
+                out=a_scales[g][:].rearrange("p k (t m) -> p t k m", t=PACK),
+                in_=scales_in.rearrange("p k (m t) -> p t k m", t=PACK),
             )
 
-        def d(g, hf, t, e):
-            xb = get(("xb", g, hf), work, [P, PACK, 2, P, 2], BF16, "xb", align_bytes=64, bufs=4)
-            dst = xb[:, t, :, :, :]
-            src = x1[g][:, t, N * hf : N * (hf + 1)].rearrange("p (w u h) -> p u w h", u=2, h=2)
-            if e == "S":
-                nc.scalar.copy(out=dst, in_=src)
-            else:
-                nc.vector.tensor_copy(out=dst, in_=src)
+        xq = [kept([P, C], U32, f"xq_{g}") for g in range(GROUPS)]
+        xq_scales = [kept([P, C], U8, f"xq_scales_{g}") for g in range(GROUPS)]
 
-        def T(g, hf, q, e):
-            bank = open_bank(("T", g, hf, q), [P, 2, 2, P])
-            xb = made[("xb", g, hf)]
-            for t in range(2):
-                for u in range(2):
-                    words = xb[:, 2 * q + t, u, :, :].rearrange("p w h -> p (w h)").bitcast(F32)
-                    nc.tensor.transpose(bank[:, t, u, :], words, ident[:])
+        def interleave_x(engine, g, half, part):
+            grouped = stage("x_grouped", (g, half), [P, HALF, PACK], 3)
+            cols = slice(PART * part, PART * (part + 1))
+            copy(engine, grouped[:, cols, :], x_in[g][half][:, :, cols].rearrange("p t c -> p c t"))
 
-        def e(g, hf, q, e):
-            grouped = get(("x1gr", g, hf), work, [P, KP, PACK], BF16, "x1gr", align_bytes=64, bufs=3)
-            dst = grouped[:, 2 * P * q : 2 * P * (q + 1), :].rearrange("p r v -> p (r v)").bitcast(F32)
-            dst = dst.rearrange("p (t r u) -> p t r u", t=2, u=2)
-            src = close_bank(("T", g, hf, q))[:].rearrange("p t u r -> p t r u")
-            if e == "S":
-                nc.scalar.copy(out=dst, in_=src)
-            else:
-                nc.vector.tensor_copy(out=dst, in_=src)
-
-        def f(g, hf, e):
+        def quantise_x(g, half):
+            cols = slice(HALF * half, HALF * (half + 1))
             nc.vector.quantize_mx(
-                out=x1q[g][hf][:].bitcast(FP8X4),
-                scales=x1s[g][hf][:],
-                in_=made[("x1gr", g, hf)][:].rearrange("p c t -> p (c t)"),
+                out=xq[g][:, cols].bitcast(FP8X4),
+                scales=xq_scales[g][:, cols],
+                in_=flat(staged["x_grouped", (g, half)]),
             )
 
-        def S2(g, hf, t, e):
-            acc = open_bank((2, g, hf, t), [P, N])
-            for kk in range(CG):
-                nc.tensor.matmul_mx(
-                    out=acc[:],
-                    lhsT=x1q[g][kk][:, P * t : P * (t + 1)].bitcast(FP8X4),
-                    lhsT_scale=x1s[g][kk][:, P * t : P * (t + 1)],
-                    rhs=r_w[:, kk, 2 * N * hf : 2 * N * (hf + 1)].bitcast(FP4X4),
-                    rhs_scale=r_sc[:, kk, N * hf : N * (hf + 1)],
-                    start=(kk == 0),
-                    stop=(kk == CG - 1),
+        x1 = [kept([P, PACK, C], F32, f"x1_{g}") for g in range(GROUPS)]
+
+        def multiply_a_pass(g, half, t, k):
+            cols = slice(HALF * half, HALF * (half + 1))
+            if k == 0:
+                open_bank((1, g, half, t), [P, HALF])
+            nc.tensor.matmul_mx(
+                out=open_banks[1, g, half, t][1][:],
+                lhsT=a_words[g][:, k, E2M1_BYTES * P * t : E2M1_BYTES * P * (t + 1)].bitcast(FP4X4),
+                lhsT_scale=a_scales[g][:, k, P * t : P * (t + 1)],
+                rhs=xq[k][:, cols].bitcast(FP8X4),
+                rhs_scale=xq_scales[k][:, cols],
+                start=(k == 0),
+                stop=(k == GROUPS - 1),
+            )
+
+        def multiply_a(g, half, pair):
+            for t in (2 * pair, 2 * pair + 1):
+                for k in range(GROUPS):
+                    multiply_a_pass(g, half, t, k)
+
+        def add_x(g, half, pair):
+            for t in (2 * pair, 2 * pair + 1):
+                nc.vector.tensor_tensor(
+                    out=x1[g][:, t, HALF * half : HALF * (half + 1)],
+                    in0=close_bank((1, g, half, t))[:],
+                    in1=x_in[g][half][:, t, :],
+                    op=ADD,
                 )
 
-        def g(g, hf, t, e):
-            x2 = get(("x2", g, hf), work, [P, PACK, N], BF16, "x2", align_bytes=64, bufs=3)
-            nc.vector.scalar_tensor_tensor(
-                out=x2[:, t, :],
-                in0=close_bank((2, g, hf, t))[:],
-                scalar=prop[:, g, t : t + 1],
-                in1=x1[g][:, t, N * hf : N * (hf + 1)],
-                op0=MULT,
-                op1=ADD,
+        x1q = [[kept([P, K_PASS], U32, f"x1q_{g}_{half}") for half in range(HALVES)] for g in range(GROUPS)]
+        x1q_scales = [[kept([P, K_PASS], U8, f"x1q_scales_{g}_{half}") for half in range(HALVES)] for g in range(GROUPS)]
+
+        def round_x1(g, half, pair):
+            rounded = stage("x1_rounded", (g, half), [P, PACK, 2, P, 2], 4)
+            for t in (2 * pair, 2 * pair + 1):
+                row = x1[g][:, t, HALF * half : HALF * (half + 1)]
+                nc.scalar.copy(out=rounded[:, t, :, :, :], in_=row.rearrange("p (w u e) -> p u w e", u=2, e=2))
+
+        def turn_x1(g, half, pair):
+            rounded = staged["x1_rounded", (g, half)]
+            turned = open_bank(("turn", g, half, pair), [P, 2, 2, P])
+            for i in range(2):
+                for u in range(2):
+                    words = rounded[:, 2 * pair + i, u, :, :].rearrange("p w e -> p (w e)").bitcast(F32)
+                    nc.tensor.transpose(turned[:, i, u, :], words, identity[:])
+
+        def regroup_x1(g, half, pair):
+            grouped = stage("x1_grouped", (g, half), [P, K_PASS, PACK], 3)
+            words = grouped[:, 2 * P * pair : 2 * P * (pair + 1), :].rearrange("p m v -> p (m v)").bitcast(F32)
+            nc.scalar.copy(
+                out=words.rearrange("p (i m u) -> p i m u", i=2, u=2),
+                in_=close_bank(("turn", g, half, pair))[:].rearrange("p i u m -> p i m u"),
             )
 
-        x2q = [kt([P, C], U32, f"x2q_{g}") for g in range(HG)]
-        x2s = [kt([P, C], U8, f"x2s_{g}") for g in range(HG)]
-
-        def h(g, hf, i, e):
-            grouped = get(("x2gr", g, hf), work, [P, N, PACK], BF16, "x2gr", align_bytes=64, bufs=2)
-            cols = slice(2 * P * i, 2 * P * (i + 1))
-            interleave(e, grouped[:, cols, :], made[("x2", g, hf)][:, :, cols].rearrange("p t c -> p c t"))
-
-        def i(g, hf, e):
+        def quantise_x1(g, half):
             nc.vector.quantize_mx(
-                out=x2q[g][:, N * hf : N * (hf + 1)].bitcast(FP8X4),
-                scales=x2s[g][:, N * hf : N * (hf + 1)],
-                in_=made[("x2gr", g, hf)][:].rearrange("p c t -> p (c t)"),
+                out=x1q[g][half][:].bitcast(FP8X4),
+                scales=x1q_scales[g][half][:],
+                in_=flat(staged["x1_grouped", (g, half)]),
             )
 
-        def S3(hf, j, kk, e):
-            if kk == 0:
-                open_bank((3, hf, j), [P, N])
-            nc.tensor.matmul_mx(
-                out=banks[(3, hf, j)][0][:],
-                lhsT=b_w[:, kk, 2 * P * j : 2 * P * (j + 1)].bitcast(FP4X4),
-                lhsT_scale=b_sc[:, kk, P * j : P * (j + 1)],
-                rhs=x2q[kk][:, N * hf : N * (hf + 1)].bitcast(FP8X4),
-                rhs_scale=x2s[kk][:, N * hf : N * (hf + 1)],
-                start=(kk == 0),
-                stop=(kk == HG - 1),
+        def multiply_r(g, half, pair):
+            for t in (2 * pair, 2 * pair + 1):
+                acc = open_bank((2, g, half, t), [P, HALF])
+                for k in range(HALVES):
+                    nc.tensor.matmul_mx(
+                        out=acc[:],
+                        lhsT=x1q[g][k][:, P * t : P * (t + 1)].bitcast(FP8X4),
+                        lhsT_scale=x1q_scales[g][k][:, P * t : P * (t + 1)],
+                        rhs=r_words[:, k, E2M1_BYTES * HALF * half : E2M1_BYTES * HALF * (half + 1)].bitcast(FP4X4),
+                        rhs_scale=r_scales[:, k, HALF * half : HALF * (half + 1)],
+                        start=(k == 0),
+                        stop=(k == HALVES - 1),
+                    )
+
+        def add_x1(g, half, pair):
+            x2 = stage("x2", (g, half), [P, PACK, HALF], 3)
+            for t in (2 * pair, 2 * pair + 1):
+                nc.vector.scalar_tensor_tensor(
+                    out=x2[:, t, :],
+                    in0=close_bank((2, g, half, t))[:],
+                    scalar=prop[:, g, t : t + 1],
+                    in1=x1[g][:, t, HALF * half : HALF * (half + 1)],
+                    op0=MULT,
+                    op1=ADD,
+                )
+
+        x2q = [kept([P, C], U32, f"x2q_{g}") for g in range(GROUPS)]
+        x2q_scales = [kept([P, C], U8, f"x2q_scales_{g}") for g in range(GROUPS)]
+
+        def interleave_x2(engine, g, half, part):
+            grouped = stage("x2_grouped", (g, half), [P, HALF, PACK], 2)
+            cols = slice(PART * part, PART * (part + 1))
+            copy(engine, grouped[:, cols, :], staged["x2", (g, half)][:, :, cols].rearrange("p t c -> p c t"))
+
+        def quantise_x2(g, half):
+            cols = slice(HALF * half, HALF * (half + 1))
+            nc.vector.quantize_mx(
+                out=x2q[g][:, cols].bitcast(FP8X4),
+                scales=x2q_scales[g][:, cols],
+                in_=flat(staged["x2_grouped", (g, half)]),
             )
 
-        def j(hf, j, e):
-            o = work.tile([P, N], F32, name="o", bufs=7)
-            nc.vector.tensor_tensor(
-                out=o[:],
-                in0=close_bank((3, hf, j))[:],
-                in1=rate_t[:, j, N * hf : N * (hf + 1)],
-                op=MULT,
-            )
-            nc.sync.dma_start(out=out[P * j : P * (j + 1), N * hf : N * (hf + 1)], in_=o[:])
+        def multiply_b(half, k):
+            cols = slice(HALF * half, HALF * (half + 1))
+            for j in range(OUT_TILES):
+                if k == 0:
+                    open_bank((3, half, j), [P, HALF])
+                nc.tensor.matmul_mx(
+                    out=open_banks[3, half, j][1][:],
+                    lhsT=b_words[:, k, E2M1_BYTES * P * j : E2M1_BYTES * P * (j + 1)].bitcast(FP4X4),
+                    lhsT_scale=b_scales[:, k, P * j : P * (j + 1)],
+                    rhs=x2q[k][:, cols].bitcast(FP8X4),
+                    rhs_scale=x2q_scales[k][:, cols],
+                    start=(k == 0),
+                    stop=(k == GROUPS - 1),
+                )
 
-        ctx.enter_context(tc.manual_schedule())
-        a(0, 0, 1, "V")
-        a(0, 0, 0, "S")
-        a(1, 0, 1, "S")
-        a(1, 0, 0, "V")
-        b(0, 0, "V")
-        b(1, 0, "V")
-        k(0, 0, "V")
-        a(2, 0, 1, "V")
-        S1(0, 0, 1, 0, "PE")
-        k(0, 1, "V")
-        a(2, 0, 0, "S")
-        a(0, 1, 0, "S")
-        S1(0, 0, 3, 0, "PE")
-        S1(0, 0, 2, 0, "PE")
-        S1(0, 0, 3, 1, "PE")
-        a(0, 1, 1, "S")
-        b(2, 0, "V")
-        a(1, 1, 0, "S")
-        S1(0, 0, 3, 2, "PE")
-        k(1, 1, "V")
-        S1(0, 0, 1, 1, "PE")
-        k(1, 0, "V")
-        S1(0, 0, 0, 0, "PE")
-        a(1, 1, 1, "S")
-        a(2, 1, 0, "S")
-        S1(0, 0, 2, 1, "PE")
-        S1(1, 0, 2, 0, "PE")
-        S1(1, 0, 2, 1, "PE")
-        S1(1, 0, 2, 2, "PE")
-        S1(0, 0, 1, 2, "PE")
-        a(2, 1, 1, "S")
-        S1(0, 0, 0, 1, "PE")
-        S1(0, 0, 0, 2, "PE")
-        S1(1, 0, 3, 0, "PE")
-        S1(1, 0, 1, 0, "PE")
-        S1(1, 0, 1, 1, "PE")
-        S1(1, 0, 1, 2, "PE")
-        b(0, 1, "V")
-        c(0, 0, 1, "V")
-        c(0, 0, 3, "V")
-        S1(1, 0, 0, 0, "PE")
-        S1(1, 0, 0, 1, "PE")
-        c(1, 0, 2, "V")
-        S1(1, 0, 3, 1, "PE")
-        S1(1, 1, 2, 0, "PE")
-        S1(0, 1, 1, 0, "PE")
-        b(1, 1, "V")
-        c(0, 0, 0, "V")
-        S1(1, 0, 3, 2, "PE")
-        d(0, 0, 1, "S")
-        S1(0, 1, 0, 0, "PE")
-        S1(0, 1, 1, 1, "PE")
-        d(0, 0, 0, "S")
-        S1(0, 1, 0, 1, "PE")
-        c(1, 0, 1, "V")
-        c(1, 0, 3, "V")
-        S1(0, 0, 2, 2, "PE")
-        c(0, 0, 2, "V")
-        S1(0, 1, 3, 0, "PE")
-        S1(1, 0, 0, 2, "PE")
-        S1(0, 1, 3, 1, "PE")
-        d(0, 0, 3, "S")
-        c(1, 0, 0, "V")
-        d(0, 0, 2, "S")
-        S1(0, 1, 2, 0, "PE")
-        S1(1, 1, 3, 0, "PE")
-        b(2, 1, "V")
-        S1(1, 1, 2, 1, "PE")
-        S1(0, 1, 2, 1, "PE")
-        T(0, 0, 0, "PE")
-        k(2, 0, "V")
-        e(0, 0, 0, "S")
-        T(0, 0, 1, "PE")
-        S1(0, 1, 3, 2, "PE")
-        S1(1, 1, 3, 1, "PE")
-        S1(1, 1, 3, 2, "PE")
-        S1(0, 1, 1, 2, "PE")
-        c(0, 1, 3, "V")
-        S1(0, 1, 2, 2, "PE")
-        S1(0, 1, 0, 2, "PE")
-        k(2, 1, "V")
-        d(1, 0, 2, "S")
-        S1(2, 1, 1, 0, "PE")
-        c(0, 1, 2, "V")
-        e(0, 0, 1, "S")
-        S1(2, 0, 1, 0, "PE")
-        S1(2, 1, 1, 1, "PE")
-        S1(1, 1, 2, 2, "PE")
-        c(0, 1, 0, "V")
-        S1(2, 0, 1, 1, "PE")
-        S1(2, 1, 1, 2, "PE")
-        S1(2, 0, 1, 2, "PE")
-        c(1, 1, 3, "V")
-        S1(2, 0, 2, 0, "PE")
-        c(0, 1, 1, "V")
-        S1(1, 1, 1, 0, "PE")
-        c(1, 1, 2, "V")
-        S1(2, 0, 0, 0, "PE")
-        S1(1, 1, 1, 1, "PE")
-        d(1, 0, 1, "S")
-        d(1, 0, 0, "S")
-        S1(1, 1, 0, 0, "PE")
-        S1(1, 1, 0, 1, "PE")
-        d(1, 0, 3, "S")
-        d(0, 1, 0, "S")
-        d(0, 1, 3, "S")
-        S1(1, 1, 0, 2, "PE")
-        S1(2, 1, 3, 0, "PE")
-        S1(2, 0, 2, 1, "PE")
-        d(1, 1, 3, "S")
-        S1(1, 1, 1, 2, "PE")
-        d(0, 1, 2, "S")
-        c(1, 1, 0, "V")
-        d(1, 1, 0, "S")
-        c(2, 1, 1, "V")
-        S1(2, 0, 2, 2, "PE")
-        S1(2, 1, 3, 1, "PE")
-        c(2, 0, 2, "V")
-        c(1, 1, 1, "V")
-        S1(2, 1, 3, 2, "PE")
-        S1(2, 1, 0, 0, "PE")
-        S1(2, 1, 0, 1, "PE")
-        S1(2, 0, 0, 1, "PE")
-        f(0, 0, "V")
-        S1(2, 0, 0, 2, "PE")
-        S1(2, 1, 0, 2, "PE")
-        T(1, 0, 0, "PE")
-        T(0, 1, 1, "PE")
-        d(0, 1, 1, "S")
-        d(1, 1, 2, "S")
-        d(2, 0, 2, "S")
-        d(1, 1, 1, "S")
-        T(0, 1, 0, "PE")
-        T(1, 0, 1, "PE")
-        c(2, 1, 0, "V")
-        e(0, 1, 1, "S")
-        T(1, 1, 1, "PE")
-        e(0, 1, 0, "S")
-        S1(2, 1, 2, 0, "PE")
-        c(2, 1, 3, "V")
-        c(2, 0, 1, "V")
-        S1(2, 1, 2, 1, "PE")
-        c(2, 0, 0, "V")
-        S1(2, 1, 2, 2, "PE")
-        S1(2, 0, 3, 0, "PE")
-        e(1, 0, 0, "S")
-        f(0, 1, "V")
-        S1(2, 0, 3, 1, "PE")
-        S1(2, 0, 3, 2, "PE")
-        S2(0, 0, 3, "PE")
-        c(2, 1, 2, "V")
-        d(2, 0, 1, "S")
-        d(2, 1, 3, "S")
-        d(2, 0, 0, "S")
-        c(2, 0, 3, "V")
-        S2(0, 1, 2, "PE")
-        S2(0, 0, 2, "PE")
-        e(1, 0, 1, "S")
-        g(0, 0, 3, "V")
-        g(0, 1, 2, "V")
-        S2(0, 1, 3, "PE")
-        d(2, 1, 2, "S")
-        f(1, 0, "V")
-        g(0, 1, 3, "V")
-        e(1, 1, 1, "S")
-        d(2, 0, 3, "S")
-        T(1, 1, 0, "PE")
-        d(2, 1, 1, "S")
-        g(0, 0, 2, "V")
-        S2(0, 0, 1, "PE")
-        e(1, 1, 0, "S")
-        S2(0, 0, 0, "PE")
-        S2(0, 1, 0, "PE")
-        g(0, 0, 1, "V")
-        d(2, 1, 0, "S")
-        T(2, 0, 0, "PE")
-        e(2, 0, 0, "S")
-        f(1, 1, "V")
-        T(2, 0, 1, "PE")
-        g(0, 0, 0, "V")
-        e(2, 0, 1, "S")
-        T(2, 1, 1, "PE")
-        S2(0, 1, 1, "PE")
-        T(2, 1, 0, "PE")
-        g(0, 1, 0, "V")
-        S2(1, 0, 1, "PE")
-        e(2, 1, 1, "S")
-        e(2, 1, 0, "S")
-        f(2, 0, "V")
-        S2(1, 0, 0, "PE")
-        g(0, 1, 1, "V")
-        f(2, 1, "V")
-        g(1, 0, 1, "V")
-        S2(1, 0, 3, "PE")
-        S2(1, 1, 1, "PE")
-        g(1, 0, 0, "V")
-        S2(1, 0, 2, "PE")
-        h(0, 0, 1, "S")
-        h(0, 0, 0, "S")
-        S2(2, 0, 3, "PE")
-        h(0, 1, 1, "S")
-        h(0, 1, 0, "S")
-        g(1, 0, 3, "V")
-        g(1, 0, 2, "V")
-        g(2, 0, 3, "V")
-        S2(2, 0, 1, "PE")
-        g(2, 0, 1, "V")
-        S2(2, 0, 0, "PE")
-        i(0, 0, "V")
-        g(2, 0, 0, "V")
-        S2(2, 1, 0, "PE")
-        S2(1, 1, 3, "PE")
-        g(1, 1, 3, "V")
-        S2(2, 0, 2, "PE")
-        S3(0, 2, 0, "PE")
-        S2(2, 1, 2, "PE")
-        i(0, 1, "V")
-        h(1, 0, 1, "S")
-        S2(1, 1, 0, "PE")
-        g(2, 0, 2, "V")
-        S2(1, 1, 2, "PE")
-        g(1, 1, 0, "V")
-        S3(0, 1, 0, "PE")
-        S3(1, 0, 0, "PE")
-        h(1, 0, 0, "S")
-        g(1, 1, 1, "V")
-        i(1, 0, "V")
-        g(2, 1, 2, "V")
-        S3(0, 0, 0, "PE")
-        g(1, 1, 2, "V")
-        S2(2, 1, 1, "PE")
-        h(2, 0, 1, "S")
-        h(2, 0, 0, "S")
-        S3(0, 3, 0, "PE")
-        S3(0, 1, 1, "PE")
-        g(2, 1, 1, "V")
-        S3(0, 0, 1, "PE")
-        S2(2, 1, 3, "PE")
-        i(2, 0, "V")
-        S3(0, 0, 2, "PE")
-        g(2, 1, 0, "V")
-        h(1, 1, 0, "S")
-        S3(0, 1, 2, "PE")
-        S3(0, 2, 1, "PE")
-        S3(1, 2, 0, "PE")
-        g(2, 1, 3, "V")
-        S3(0, 2, 2, "PE")
-        h(1, 1, 1, "S")
-        S3(1, 3, 0, "PE")
-        h(2, 1, 0, "S")
-        j(0, 0, "V")
-        h(2, 1, 1, "V")
-        i(1, 1, "V")
-        i(2, 1, "V")
-        S3(0, 3, 1, "PE")
-        j(0, 1, "V")
-        S3(0, 3, 2, "PE")
-        S3(1, 1, 0, "PE")
-        j(0, 3, "V")
-        S3(1, 2, 1, "PE")
-        S3(1, 3, 1, "PE")
-        S3(1, 0, 1, "PE")
-        j(0, 2, "V")
-        S3(1, 0, 2, "PE")
-        S3(1, 2, 2, "PE")
-        j(1, 2, "V")
-        j(1, 0, "V")
-        S3(1, 3, 2, "PE")
-        S3(1, 1, 1, "PE")
-        j(1, 3, "V")
-        S3(1, 1, 2, "PE")
-        j(1, 1, "V")
+        def finish(half, pair):
+            cols = slice(HALF * half, HALF * (half + 1))
+            for j in (2 * pair, 2 * pair + 1):
+                response = work.tile([P, HALF], F32, name="response", bufs=7)
+                nc.vector.tensor_tensor(out=response[:], in0=close_bank((3, half, j))[:], in1=rates[:, j, cols], op=MULT)
+                nc.sync.dma_start(out=out[P * j : P * (j + 1), cols], in_=response[:])
+
+        reorder_a_words(0, 0)
+        reorder_a_words(0, 1)
+        interleave_x("vector", 0, 0, 1)
+        reorder_a_scales(0)
+        interleave_x("vector", 1, 0, 1)
+        interleave_x("scalar", 0, 0, 0)
+        interleave_x("scalar", 1, 0, 0)
+        interleave_x("scalar", 2, 0, 1)
+        quantise_x(0, 0)
+        interleave_x("vector", 2, 0, 0)
+        quantise_x(1, 0)
+        interleave_x("vector", 0, 1, 0)
+        quantise_x(2, 0)
+        reorder_a_words(1, 0)
+        reorder_a_scales(1)
+        reorder_a_words(1, 1)
+        interleave_x("scalar", 0, 1, 1)
+        interleave_x("scalar", 1, 1, 0)
+        interleave_x("scalar", 1, 1, 1)
+        interleave_x("scalar", 2, 1, 0)
+        for k in range(GROUPS):
+            for t in range(PACK):
+                multiply_a_pass(0, 0, t, k)
+        add_x(0, 0, 1)
+        interleave_x("vector", 2, 1, 1)
+        quantise_x(0, 1)
+        quantise_x(1, 1)
+        quantise_x(2, 1)
+        multiply_a(1, 0, 0)
+        multiply_a(1, 0, 1)
+        add_x(1, 0, 1)
+        add_x(1, 0, 0)
+        add_x(0, 0, 0)
+        round_x1(1, 0, 1)
+        round_x1(1, 0, 0)
+        round_x1(0, 0, 0)
+        round_x1(0, 0, 1)
+        multiply_a(0, 1, 1)
+        multiply_a(0, 1, 0)
+        add_x(0, 1, 0)
+        reorder_a_words(2, 0)
+        reorder_a_scales(2)
+        add_x(0, 1, 1)
+        round_x1(0, 1, 0)
+        round_x1(0, 1, 1)
+        multiply_a(1, 1, 1)
+        multiply_a(1, 1, 0)
+        add_x(1, 1, 0)
+        add_x(1, 1, 1)
+        round_x1(1, 1, 0)
+        multiply_a(2, 0, 0)
+        add_x(2, 0, 0)
+        reorder_a_words(2, 1)
+        turn_x1(1, 0, 1)
+        turn_x1(0, 1, 0)
+        turn_x1(0, 0, 1)
+        regroup_x1(0, 0, 1)
+        regroup_x1(0, 1, 0)
+        turn_x1(0, 1, 1)
+        turn_x1(1, 0, 0)
+        turn_x1(0, 0, 0)
+        regroup_x1(0, 0, 0)
+        regroup_x1(1, 0, 0)
+        regroup_x1(1, 0, 1)
+        regroup_x1(0, 1, 1)
+        round_x1(1, 1, 1)
+        round_x1(2, 0, 0)
+        multiply_a(2, 1, 0)
+        quantise_x1(0, 0)
+        add_x(2, 1, 0)
+        quantise_x1(1, 0)
+        round_x1(2, 1, 0)
+        multiply_a(2, 1, 1)
+        add_x(2, 1, 1)
+        quantise_x1(0, 1)
+        turn_x1(1, 1, 0)
+        regroup_x1(1, 1, 0)
+        turn_x1(1, 1, 1)
+        regroup_x1(1, 1, 1)
+        multiply_a(2, 0, 1)
+        add_x(2, 0, 1)
+        round_x1(2, 0, 1)
+        round_x1(2, 1, 1)
+        multiply_r(0, 1, 1)
+        add_x1(0, 1, 1)
+        quantise_x1(1, 1)
+        multiply_r(0, 1, 0)
+        add_x1(0, 1, 0)
+        turn_x1(2, 0, 1)
+        regroup_x1(2, 0, 1)
+        interleave_x2("scalar", 0, 1, 0)
+        interleave_x2("scalar", 0, 1, 1)
+        turn_x1(2, 0, 0)
+        multiply_r(1, 0, 0)
+        add_x1(1, 0, 0)
+        multiply_r(1, 0, 1)
+        add_x1(1, 0, 1)
+        interleave_x2("scalar", 1, 0, 0)
+        interleave_x2("scalar", 1, 0, 1)
+        multiply_r(0, 0, 0)
+        add_x1(0, 0, 0)
+        quantise_x2(0, 1)
+        multiply_r(1, 1, 1)
+        add_x1(1, 1, 1)
+        multiply_r(0, 0, 1)
+        add_x1(0, 0, 1)
+        quantise_x2(1, 0)
+        turn_x1(2, 1, 1)
+        regroup_x1(2, 1, 1)
+        turn_x1(2, 1, 0)
+        regroup_x1(2, 1, 0)
+        regroup_x1(2, 0, 0)
+        interleave_x2("scalar", 0, 0, 0)
+        interleave_x2("scalar", 0, 0, 1)
+        multiply_r(1, 1, 0)
+        quantise_x1(2, 1)
+        quantise_x1(2, 0)
+        add_x1(1, 1, 0)
+        interleave_x2("scalar", 1, 1, 0)
+        interleave_x2("scalar", 1, 1, 1)
+        multiply_b(1, 0)
+        multiply_r(2, 1, 1)
+        add_x1(2, 1, 1)
+        quantise_x2(0, 0)
+        multiply_r(2, 1, 0)
+        add_x1(2, 1, 0)
+        quantise_x2(1, 1)
+        interleave_x2("scalar", 2, 1, 1)
+        interleave_x2("scalar", 2, 1, 0)
+        multiply_r(2, 0, 0)
+        multiply_r(2, 0, 1)
+        add_x1(2, 0, 1)
+        add_x1(2, 0, 0)
+        quantise_x2(2, 1)
+        interleave_x2("vector", 2, 0, 0)
+        interleave_x2("scalar", 2, 0, 1)
+        multiply_b(1, 1)
+        multiply_b(0, 0)
+        multiply_b(1, 2)
+        finish(1, 0)
+        quantise_x2(2, 0)
+        finish(1, 1)
+        multiply_b(0, 1)
+        multiply_b(0, 2)
+        finish(0, 0)
+        finish(0, 1)

from contextlib import ExitStack

import concourse.mybir as mybir
from concourse.masks import make_identity

H, C, G = 1536, 1024, 512
FLOPS = 2 * (H * H * C + H * C * C + H * G * C)

F32 = mybir.dt.float32
BF16 = mybir.dt.bfloat16
I32 = mybir.dt.int32
U32 = mybir.dt.uint32
U8 = mybir.dt.uint8
FP8X4 = mybir.dt.float8_e4m3fn_x4
FP4X4 = mybir.dt.float4_e2m1fn_x4
ADD = mybir.AluOpType.add
MULT = mybir.AluOpType.mult

P = 128
PACK = 4
K_PASS = P * PACK
GROUPS = H // K_PASS
HALVES = C // K_PASS
HALF = K_PASS
PART = HALF // 2
OUT_TILES = G // P
BANKS = 8
E2M1_BYTES = 2


def tile_household_bracket_response_t2_kernel(
    tc,
    x,
    transfer_words,
    transfer_scales,
    reclass_words,
    reclass_scales,
    bracket_words,
    bracket_scales,
    propensity,
    rate,
    out,
):
    nc = tc.nc
    with ExitStack() as ctx:
        keep = ctx.enter_context(tc.tile_pool(name="keep", bufs=1))
        work = ctx.enter_context(tc.tile_pool(name="work", bufs=3))
        psum = ctx.enter_context(tc.psum_pool(name="psum", bufs=1))
        ctx.enter_context(tc.manual_schedule())

        def kept(shape, dtype, name):
            return keep.tile(shape, dtype, name=name, align_bytes=64)

        a_scales_in = [kept([P, GROUPS, K_PASS], U8, "a_scales_first"), kept([P, GROUPS, H - K_PASS], U8, "a_scales_rest")]
        r_scales = kept([P, HALVES, C], U8, "r_scales")
        b_scales = kept([P, GROUPS, G], U8, "b_scales")
        nc.vector.memset(a_scales_in[0][:].bitcast(I32), 0)
        nc.gpsimd.memset(a_scales_in[1][:].bitcast(I32), 0)
        nc.gpsimd.memset(r_scales[:].bitcast(I32), 0)
        nc.gpsimd.memset(b_scales[:].bitcast(I32), 0)
        identity = kept([P, P], F32, "identity")
        make_identity(nc, identity[:])

        def load_scales(plane, scales):
            words = plane[:].bitcast(I32)
            for q in range(4):
                nc.sync.dma_start(
                    out=words[32 * q : 32 * q + 4, :, :],
                    in_=scales[:, 4 * q : 4 * q + 4, :].rearrange("k r n -> r k n").bitcast(I32),
                )

        def load_words(tile, words):
            nc.sync.dma_start(out=tile[:].bitcast(I32), in_=words.rearrange("k p n -> p k n").bitcast(I32))

        x_in = [[kept([P, PACK, HALF], BF16, f"x_{g}_{half}") for half in range(HALVES)] for g in range(GROUPS)]
        a_in = [kept([P, GROUPS, E2M1_BYTES * K_PASS], U8, f"a_in_{g}") for g in range(GROUPS)]
        r_words = kept([P, HALVES, E2M1_BYTES * C], U8, "r_words")
        b_words = kept([P, GROUPS, E2M1_BYTES * G], U8, "b_words")
        prop = kept([P, GROUPS, PACK], BF16, "prop")
        rates = kept([P, OUT_TILES, C], BF16, "rates")

        def load_x(g, half):
            nc.sync.dma_start(
                out=x_in[g][half][:],
                in_=x[K_PASS * g : K_PASS * (g + 1), HALF * half : HALF * (half + 1)].rearrange("(p t) c -> p t c", t=PACK),
            )

        def load_a(g):
            width = E2M1_BYTES * K_PASS
            load_words(a_in[g], transfer_words[:, :, width * g : width * (g + 1)])

        load_a(0)
        load_scales(a_scales_in[0], transfer_scales[:, :, :K_PASS])
        load_x(0, 0)
        load_x(1, 0)
        load_x(2, 0)
        load_x(0, 1)
        load_scales(a_scales_in[1], transfer_scales[:, :, K_PASS:])
        load_a(1)
        load_x(1, 1)
        load_x(2, 1)
        load_a(2)
        load_scales(r_scales, reclass_scales)
        load_words(r_words, reclass_words)
        nc.sync.dma_start(out=prop[:], in_=propensity.rearrange("(g p t) -> p g t", p=P, t=PACK))
        load_scales(b_scales, bracket_scales)
        load_words(b_words, bracket_words)
        nc.sync.dma_start(out=rates[:], in_=rate.rearrange("(j p) c -> p j c", p=P))

        closed_banks = list(range(BANKS))
        open_banks = {}

        def open_bank(key, shape):
            bank = closed_banks.pop(0)
            tile = psum.tile(shape, F32, name="acc", tag=f"bank_{bank}")
            open_banks[key] = bank, tile
            return tile

        def close_bank(key):
            bank, tile = open_banks.pop(key)
            closed_banks.append(bank)
            return tile

        staged = {}

        def stage(kind, key, shape, bufs):
            if (kind, key) not in staged:
                tile = work.tile(shape, BF16, name=kind, tag=kind, bufs=bufs, align_bytes=64)
                staged[kind, key] = tile
            return staged[kind, key]

        def copy(engine, out_ap, in_ap):
            if engine == "vector":
                nc.vector.tensor_copy(out=out_ap, in_=in_ap)
            else:
                nc.scalar.copy(out=out_ap, in_=in_ap)

        def flat(tile):
            return tile[:].rearrange("p c t -> p (c t)")

        a_words = [kept([P, GROUPS, E2M1_BYTES * K_PASS], U8, f"a_words_{g}") for g in range(GROUPS)]
        a_scales = [kept([P, GROUPS, K_PASS], U8, f"a_scales_{g}") for g in range(GROUPS)]

        def reorder_a_words(g, pair):
            tiles = slice(2 * pair, 2 * pair + 2)
            nc.vector.tensor_copy(
                out=a_words[g][:].rearrange("p k (t m b) -> p t k m b", t=PACK, b=E2M1_BYTES)[:, tiles, :, :, :],
                in_=a_in[g][:].rearrange("p k (m t b) -> p t k m b", t=PACK, b=E2M1_BYTES)[:, tiles, :, :, :],
            )

        def reorder_a_scales(g):
            if g == 0:
                scales_in = a_scales_in[0][:]
            else:
                scales_in = a_scales_in[1][:, :, K_PASS * (g - 1) : K_PASS * g]
            nc.vector.tensor_copy(
                out=a_scales[g][:].rearrange("p k (t m) -> p t k m", t=PACK),
                in_=scales_in.rearrange("p k (m t) -> p t k m", t=PACK),
            )

        xq = [kept([P, C], U32, f"xq_{g}") for g in range(GROUPS)]
        xq_scales = [kept([P, C], U8, f"xq_scales_{g}") for g in range(GROUPS)]

        def interleave_x(engine, g, half, part):
            grouped = stage("x_grouped", (g, half), [P, HALF, PACK], 3)
            cols = slice(PART * part, PART * (part + 1))
            copy(engine, grouped[:, cols, :], x_in[g][half][:, :, cols].rearrange("p t c -> p c t"))

        def quantise_x(g, half):
            cols = slice(HALF * half, HALF * (half + 1))
            nc.vector.quantize_mx(
                out=xq[g][:, cols].bitcast(FP8X4),
                scales=xq_scales[g][:, cols],
                in_=flat(staged["x_grouped", (g, half)]),
            )

        x1 = [kept([P, PACK, C], F32, f"x1_{g}") for g in range(GROUPS)]

        def multiply_a_pass(g, half, t, k):
            cols = slice(HALF * half, HALF * (half + 1))
            if k == 0:
                open_bank((1, g, half, t), [P, HALF])
            nc.tensor.matmul_mx(
                out=open_banks[1, g, half, t][1][:],
                lhsT=a_words[g][:, k, E2M1_BYTES * P * t : E2M1_BYTES * P * (t + 1)].bitcast(FP4X4),
                lhsT_scale=a_scales[g][:, k, P * t : P * (t + 1)],
                rhs=xq[k][:, cols].bitcast(FP8X4),
                rhs_scale=xq_scales[k][:, cols],
                start=(k == 0),
                stop=(k == GROUPS - 1),
            )

        def multiply_a(g, half, pair):
            for t in (2 * pair, 2 * pair + 1):
                for k in range(GROUPS):
                    multiply_a_pass(g, half, t, k)

        def add_x(g, half, pair):
            for t in (2 * pair, 2 * pair + 1):
                nc.vector.tensor_tensor(
                    out=x1[g][:, t, HALF * half : HALF * (half + 1)],
                    in0=close_bank((1, g, half, t))[:],
                    in1=x_in[g][half][:, t, :],
                    op=ADD,
                )

        x1q = [[kept([P, K_PASS], U32, f"x1q_{g}_{half}") for half in range(HALVES)] for g in range(GROUPS)]
        x1q_scales = [[kept([P, K_PASS], U8, f"x1q_scales_{g}_{half}") for half in range(HALVES)] for g in range(GROUPS)]

        def round_x1(g, half, pair):
            rounded = stage("x1_rounded", (g, half), [P, PACK, 2, P, 2], 4)
            for t in (2 * pair, 2 * pair + 1):
                row = x1[g][:, t, HALF * half : HALF * (half + 1)]
                nc.scalar.copy(out=rounded[:, t, :, :, :], in_=row.rearrange("p (w u e) -> p u w e", u=2, e=2))

        def turn_x1(g, half, pair):
            rounded = staged["x1_rounded", (g, half)]
            turned = open_bank(("turn", g, half, pair), [P, 2, 2, P])
            for i in range(2):
                for u in range(2):
                    words = rounded[:, 2 * pair + i, u, :, :].rearrange("p w e -> p (w e)").bitcast(F32)
                    nc.tensor.transpose(turned[:, i, u, :], words, identity[:])

        def regroup_x1(g, half, pair):
            grouped = stage("x1_grouped", (g, half), [P, K_PASS, PACK], 3)
            words = grouped[:, 2 * P * pair : 2 * P * (pair + 1), :].rearrange("p m v -> p (m v)").bitcast(F32)
            nc.scalar.copy(
                out=words.rearrange("p (i m u) -> p i m u", i=2, u=2),
                in_=close_bank(("turn", g, half, pair))[:].rearrange("p i u m -> p i m u"),
            )

        def quantise_x1(g, half):
            nc.vector.quantize_mx(
                out=x1q[g][half][:].bitcast(FP8X4),
                scales=x1q_scales[g][half][:],
                in_=flat(staged["x1_grouped", (g, half)]),
            )

        def multiply_r(g, half, pair):
            for t in (2 * pair, 2 * pair + 1):
                acc = open_bank((2, g, half, t), [P, HALF])
                for k in range(HALVES):
                    nc.tensor.matmul_mx(
                        out=acc[:],
                        lhsT=x1q[g][k][:, P * t : P * (t + 1)].bitcast(FP8X4),
                        lhsT_scale=x1q_scales[g][k][:, P * t : P * (t + 1)],
                        rhs=r_words[:, k, E2M1_BYTES * HALF * half : E2M1_BYTES * HALF * (half + 1)].bitcast(FP4X4),
                        rhs_scale=r_scales[:, k, HALF * half : HALF * (half + 1)],
                        start=(k == 0),
                        stop=(k == HALVES - 1),
                    )

        def add_x1(g, half, pair):
            x2 = stage("x2", (g, half), [P, PACK, HALF], 3)
            for t in (2 * pair, 2 * pair + 1):
                nc.vector.scalar_tensor_tensor(
                    out=x2[:, t, :],
                    in0=close_bank((2, g, half, t))[:],
                    scalar=prop[:, g, t : t + 1],
                    in1=x1[g][:, t, HALF * half : HALF * (half + 1)],
                    op0=MULT,
                    op1=ADD,
                )

        x2q = [kept([P, C], U32, f"x2q_{g}") for g in range(GROUPS)]
        x2q_scales = [kept([P, C], U8, f"x2q_scales_{g}") for g in range(GROUPS)]

        def interleave_x2(engine, g, half, part):
            grouped = stage("x2_grouped", (g, half), [P, HALF, PACK], 2)
            cols = slice(PART * part, PART * (part + 1))
            copy(engine, grouped[:, cols, :], staged["x2", (g, half)][:, :, cols].rearrange("p t c -> p c t"))

        def quantise_x2(g, half):
            cols = slice(HALF * half, HALF * (half + 1))
            nc.vector.quantize_mx(
                out=x2q[g][:, cols].bitcast(FP8X4),
                scales=x2q_scales[g][:, cols],
                in_=flat(staged["x2_grouped", (g, half)]),
            )

        def multiply_b(half, k):
            cols = slice(HALF * half, HALF * (half + 1))
            for j in range(OUT_TILES):
                if k == 0:
                    open_bank((3, half, j), [P, HALF])
                nc.tensor.matmul_mx(
                    out=open_banks[3, half, j][1][:],
                    lhsT=b_words[:, k, E2M1_BYTES * P * j : E2M1_BYTES * P * (j + 1)].bitcast(FP4X4),
                    lhsT_scale=b_scales[:, k, P * j : P * (j + 1)],
                    rhs=x2q[k][:, cols].bitcast(FP8X4),
                    rhs_scale=x2q_scales[k][:, cols],
                    start=(k == 0),
                    stop=(k == GROUPS - 1),
                )

        def finish(half, pair):
            cols = slice(HALF * half, HALF * (half + 1))
            for j in (2 * pair, 2 * pair + 1):
                response = work.tile([P, HALF], F32, name="response", bufs=7)
                nc.vector.tensor_tensor(out=response[:], in0=close_bank((3, half, j))[:], in1=rates[:, j, cols], op=MULT)
                nc.sync.dma_start(out=out[P * j : P * (j + 1), cols], in_=response[:])

        reorder_a_words(0, 0)
        reorder_a_words(0, 1)
        interleave_x("vector", 0, 0, 1)
        reorder_a_scales(0)
        interleave_x("vector", 1, 0, 1)
        interleave_x("scalar", 0, 0, 0)
        interleave_x("scalar", 1, 0, 0)
        interleave_x("scalar", 2, 0, 1)
        quantise_x(0, 0)
        interleave_x("vector", 2, 0, 0)
        quantise_x(1, 0)
        interleave_x("vector", 0, 1, 0)
        quantise_x(2, 0)
        reorder_a_words(1, 0)
        reorder_a_scales(1)
        reorder_a_words(1, 1)
        interleave_x("scalar", 0, 1, 1)
        interleave_x("scalar", 1, 1, 0)
        interleave_x("scalar", 1, 1, 1)
        interleave_x("scalar", 2, 1, 0)
        for k in range(GROUPS):
            for t in range(PACK):
                multiply_a_pass(0, 0, t, k)
        add_x(0, 0, 1)
        interleave_x("vector", 2, 1, 1)
        quantise_x(0, 1)
        quantise_x(1, 1)
        quantise_x(2, 1)
        multiply_a(1, 0, 0)
        multiply_a(1, 0, 1)
        add_x(1, 0, 1)
        add_x(1, 0, 0)
        add_x(0, 0, 0)
        round_x1(1, 0, 1)
        round_x1(1, 0, 0)
        round_x1(0, 0, 0)
        round_x1(0, 0, 1)
        multiply_a(0, 1, 1)
        multiply_a(0, 1, 0)
        add_x(0, 1, 0)
        reorder_a_words(2, 0)
        reorder_a_scales(2)
        add_x(0, 1, 1)
        round_x1(0, 1, 0)
        round_x1(0, 1, 1)
        multiply_a(1, 1, 1)
        multiply_a(1, 1, 0)
        add_x(1, 1, 0)
        add_x(1, 1, 1)
        round_x1(1, 1, 0)
        multiply_a(2, 0, 0)
        add_x(2, 0, 0)
        reorder_a_words(2, 1)
        turn_x1(1, 0, 1)
        turn_x1(0, 1, 0)
        turn_x1(0, 0, 1)
        regroup_x1(0, 0, 1)
        regroup_x1(0, 1, 0)
        turn_x1(0, 1, 1)
        turn_x1(1, 0, 0)
        turn_x1(0, 0, 0)
        regroup_x1(0, 0, 0)
        regroup_x1(1, 0, 0)
        regroup_x1(1, 0, 1)
        regroup_x1(0, 1, 1)
        round_x1(1, 1, 1)
        round_x1(2, 0, 0)
        multiply_a(2, 1, 0)
        quantise_x1(0, 0)
        add_x(2, 1, 0)
        quantise_x1(1, 0)
        round_x1(2, 1, 0)
        multiply_a(2, 1, 1)
        add_x(2, 1, 1)
        quantise_x1(0, 1)
        turn_x1(1, 1, 0)
        regroup_x1(1, 1, 0)
        turn_x1(1, 1, 1)
        regroup_x1(1, 1, 1)
        multiply_a(2, 0, 1)
        add_x(2, 0, 1)
        round_x1(2, 0, 1)
        round_x1(2, 1, 1)
        multiply_r(0, 1, 1)
        add_x1(0, 1, 1)
        quantise_x1(1, 1)
        multiply_r(0, 1, 0)
        add_x1(0, 1, 0)
        turn_x1(2, 0, 1)
        regroup_x1(2, 0, 1)
        interleave_x2("scalar", 0, 1, 0)
        interleave_x2("scalar", 0, 1, 1)
        turn_x1(2, 0, 0)
        multiply_r(1, 0, 0)
        add_x1(1, 0, 0)
        multiply_r(1, 0, 1)
        add_x1(1, 0, 1)
        interleave_x2("scalar", 1, 0, 0)
        interleave_x2("scalar", 1, 0, 1)
        multiply_r(0, 0, 0)
        add_x1(0, 0, 0)
        quantise_x2(0, 1)
        multiply_r(1, 1, 1)
        add_x1(1, 1, 1)
        multiply_r(0, 0, 1)
        add_x1(0, 0, 1)
        quantise_x2(1, 0)
        turn_x1(2, 1, 1)
        regroup_x1(2, 1, 1)
        turn_x1(2, 1, 0)
        regroup_x1(2, 1, 0)
        regroup_x1(2, 0, 0)
        interleave_x2("scalar", 0, 0, 0)
        interleave_x2("scalar", 0, 0, 1)
        multiply_r(1, 1, 0)
        quantise_x1(2, 1)
        quantise_x1(2, 0)
        add_x1(1, 1, 0)
        interleave_x2("scalar", 1, 1, 0)
        interleave_x2("scalar", 1, 1, 1)
        multiply_b(1, 0)
        multiply_r(2, 1, 1)
        add_x1(2, 1, 1)
        quantise_x2(0, 0)
        multiply_r(2, 1, 0)
        add_x1(2, 1, 0)
        quantise_x2(1, 1)
        interleave_x2("scalar", 2, 1, 1)
        interleave_x2("scalar", 2, 1, 0)
        multiply_r(2, 0, 0)
        multiply_r(2, 0, 1)
        add_x1(2, 0, 1)
        add_x1(2, 0, 0)
        quantise_x2(2, 1)
        interleave_x2("vector", 2, 0, 0)
        interleave_x2("scalar", 2, 0, 1)
        multiply_b(1, 1)
        multiply_b(0, 0)
        multiply_b(1, 2)
        finish(1, 0)
        quantise_x2(2, 0)
        finish(1, 1)
        multiply_b(0, 1)
        multiply_b(0, 2)
        finish(0, 0)
        finish(0, 1)
